import numpy as np
import ml_dtypes


def mxq(x, axis, fmt="e4m3"):
    dtype, down = {"e4m3": (ml_dtypes.float8_e4m3fn, 7), "e5m2": (ml_dtypes.float8_e5m2, 14)}[fmt]
    v = np.moveaxis(np.asarray(x, np.float32).astype(ml_dtypes.bfloat16).astype(np.float64), axis, -1)
    blocks = v.reshape(v.shape[:-1] + (-1, 32))
    amax = np.abs(blocks).max(-1, keepdims=True)
    byte = np.maximum(np.where(amax > 0, np.frexp(amax)[1] - 1 + 127, 0) - down, 1)
    scale = np.exp2(byte - 127.0)
    codes = (blocks / scale).astype(np.float32).astype(dtype).astype(np.float64)
    return np.moveaxis((codes * scale).reshape(v.shape), -1, axis)


WIDE = False


def mx_kscale(k):
    if not WIDE:
        return np.ones(k)
    levels = np.array([10, -10, 5, -5, 0])
    if k % 512:
        return np.exp2(np.random.permutation(np.resize(levels, k // 32))).repeat(32)
    a = np.empty((k // 512, 16))
    for p in range(k // 512):
        a[p, :8] = np.random.permutation(np.resize(levels, 8))
        for g in range(8):
            far = levels[np.abs(levels - a[p, g]) >= 10]
            a[p, g + 8] = far[np.random.randint(len(far))]
    return np.exp2(a.ravel()).repeat(32)


BF16 = ml_dtypes.bfloat16


def bf(x):
    return np.asarray(x, np.float32).astype(BF16)


def f64(x):
    return np.asarray(x).astype(np.float64)


E2M1 = np.array([0.0, 0.5, 1.0, 1.5, 2.0, 3.0, 4.0, 6.0, -0.0, -0.5, -1.0, -1.5, -2.0, -3.0, -4.0, -6.0])


def pack_weight(w, fmt):
    k, n = w.shape
    w = f64(bf(w)).reshape(k // 32, 32, n)
    amax = np.abs(w).max(1)
    if fmt == "e4m3":
        byte = np.frexp(amax)[1] - 1 + 127 - 7
    else:
        mant, ex = np.frexp(amax / 6.0)
        byte = np.where(mant > 0.5, ex, ex - 1) + 127
    byte = np.clip(np.where(amax > 0, byte, 1), 1, 254)
    scaled = (w * np.exp2(127.0 - byte)[:, None, :]).reshape(k, n).astype(np.float32)
    by_word = np.ascontiguousarray(scaled.reshape(k // 512, 128, 4, n).transpose(0, 1, 3, 2))
    if fmt == "e4m3":
        words = by_word.astype(ml_dtypes.float8_e4m3fn).view(np.uint8)
    else:
        c = by_word.astype(ml_dtypes.float4_e2m1fn).view(np.uint8) & 0xF
        words = c[..., 0::2] | (c[..., 1::2] << 4)
    return np.ascontiguousarray(words), np.ascontiguousarray(byte.astype(np.uint8).reshape(k // 512, 16, n))


def unpack_weight(words, scales, fmt):
    g, p, n, _ = words.shape
    if fmt == "e4m3":
        vals = np.ascontiguousarray(words).view(ml_dtypes.float8_e4m3fn).astype(np.float64)
    else:
        nib = np.empty((g, p, n, 4), np.uint8)
        nib[..., 0::2] = words & 0xF
        nib[..., 1::2] = words >> 4
        vals = E2M1[nib]
    vals = vals * np.repeat(np.exp2(scales.astype(np.float64) - 127.0), 8, axis=1)[..., None]
    return vals.transpose(0, 1, 3, 2).reshape(g * 512, n)
def pack4(w):
    words, scales = pack_weight(w, "e2m1")
    return words.reshape(words.shape[0], 128, -1), scales


def unpack4(words, scales):
    return unpack_weight(words.reshape(words.shape[0], 128, -1, 2), scales, "e2m1")


E4M3FN = np.array([(-1.0 if i & 128 else 1.0) * ((1.0 + (i & 7) / 8.0) * 2.0 ** (((i >> 3) & 15) - 7) if i & 120 else (i & 7) * 2.0 ** -9) for i in range(256)])


def e4m3fn_bytes(y):
    return np.clip(np.asarray(y, np.float64), -448.0, 448.0).astype(np.float32).astype(ml_dtypes.float8_e4m3fn).view(np.uint8)


def e4m3fn_values(b):
    return E4M3FN[b]


T, K, J, D, B = 1024, 1024, 2048, 1024, 128


def setup_inputs():
    s, t = mx_kscale(K), mx_kscale(J)
    sigma = (0.5 / K) ** 0.25
    x = np.random.standard_normal((T, K)) * sigma
    c = np.random.standard_normal((J, K)) * sigma
    mean = K * sigma ** 2 / 2
    row = np.exp(mean - (x ** 2).sum(1) / 2)
    amp = np.exp(mean - (c ** 2).sum(1) / 2)
    x = x * s
    x_scale = (np.abs(x).reshape(T, K // B, B).max(2) / 448.0).astype(np.float32)
    w_words, w_scales = pack4(np.random.standard_normal((J, D)) / np.sqrt(J) / t[:, None])
    return {"X_bytes": e4m3fn_bytes(x / np.repeat(f64(x_scale), B, axis=1)),
            "X_scale": x_scale,
            "C": bf(c / s),
            "amp": bf(amp * t),
            "row": bf(row),
            "W_words": w_words,
            "W_scales": w_scales}


def reference(X_bytes, X_scale, C, amp, row, W_words, W_scales):
    x = e4m3fn_values(X_bytes) * np.repeat(f64(X_scale), B, axis=1)
    z = mxq(x, 1, "e4m3") @ mxq(f64(C), 1, "e4m3").T
    h = np.exp(z) * f64(amp)
    y = mxq(h, 1, "e4m3") @ unpack4(W_words, W_scales)
    return y * f64(row)[:, None]

@@ -1,0 +1,339 @@
+from contextlib import ExitStack
+
+import concourse.mybir as mybir
+from concourse.masks import make_identity
+
+T, K, J, D = 1024, 1024, 2048, 1024
+FLOPS = 2 * T * K * J + 2 * T * J * D
+
+F32 = mybir.dt.float32
+BF16 = mybir.dt.bfloat16
+U32 = mybir.dt.uint32
+I32 = mybir.dt.int32
+U8 = mybir.dt.uint8
+F8 = mybir.dt.float8_e4m3fn
+FP8X4 = mybir.dt.float8_e4m3fn_x4
+FP4X4 = mybir.dt.float4_e2m1fn_x4
+MULT = mybir.AluOpType.mult
+EXP = mybir.ActivationFunctionType.Exp
+COPY = mybir.ActivationFunctionType.Copy
+
+P = 128
+NT = T // P
+NQ = 4
+QT = T // NQ
+NG = J // 512
+
+
+def tile_rbf_kernel_readout_d4_kernel(tc, X_bytes, X_scale, C, amp, row, W_words, W_scales, out):
+    nc = tc.nc
+    with ExitStack() as ctx:
+        keep = ctx.enter_context(tc.tile_pool(name="keep", bufs=1))
+        stage = ctx.enter_context(tc.tile_pool(name="stage", bufs=3))
+        psum = ctx.enter_context(tc.psum_pool(name="psum", bufs=8))
+        ctx.enter_context(tc.manual_schedule())
+
+        ident = keep.tile([P, P], F32, name="ident")
+        x_raw = [keep.tile([P, 2, K], U8, name="x_raw%d" % q) for q in range(NQ)]
+        x_sc = keep.tile([P, NT, 8], F32, name="x_sc")
+        c_raw = [keep.tile([P, 4, K], BF16, name="c_raw%d" % g) for g in range(NG)]
+        amp_sb = keep.tile([P, NG, 4], BF16, name="amp_sb")
+        row_bf = keep.tile([P, NT], BF16, name="row_bf")
+        row_sb = keep.tile([P, NT], F32, name="row_sb")
+        w_sb = keep.tile([P, NG, 2 * D], U8, name="w_sb", align_bytes=64)
+        w_sc = keep.tile([P, NG, D], U8, name="w_sc", align_bytes=64)
+        x_codes = [keep.tile([P, 2, QT], U32, name="x_codes%d" % q, align_bytes=64) for q in range(NQ)]
+        x_planes = [keep.tile([P, 2, QT], U8, name="x_planes%d" % q, align_bytes=64) for q in range(NQ)]
+        c_codes = [keep.tile([P, 2, P], U32, name="c_codes%d" % c, align_bytes=64) for c in range(4 * NG)]
+        c_planes = [keep.tile([P, 2, P], U8, name="c_planes%d" % c, align_bytes=64) for c in range(4 * NG)]
+        h_codes = [[keep.tile([P, QT], U32, name="h_codes%d_%d" % (q, g), align_bytes=64) for g in range(NG)] for q in range(NQ)]
+        h_planes = [[keep.tile([P, QT], U8, name="h_planes%d_%d" % (q, g), align_bytes=64) for g in range(NG)] for q in range(NQ)]
+
+        make_identity(nc, ident[:])
+
+        x_view = X_bytes.rearrange("(p i) k -> p i k", i=NT)
+        c_view = C.rearrange("(g m t) k -> g m t k", g=NG, t=4)
+        nc.sync.dma_start(out=c_raw[0][:, 0:1, :], in_=c_view[0][:, 0:1, :])
+        nc.sync.dma_start(out=x_sc[:], in_=X_scale.rearrange("(p i) b -> p i b", i=NT))
+        nc.sync.dma_start(out=x_raw[0][:], in_=x_view[:, 0:2, :])
+        for t in range(1, 4):
+            nc.sync.dma_start(out=c_raw[0][:, t : t + 1, :], in_=c_view[0][:, t : t + 1, :])
+        nc.sync.dma_start(out=amp_sb[:], in_=amp.rearrange("(g m t) -> m g t", g=NG, t=4))
+        for g in range(1, NG):
+            for t in (0, 2):
+                nc.sync.dma_start(out=c_raw[g][:, t : t + 2, :], in_=c_view[g][:, t : t + 2, :])
+            if g == 1:
+                nc.sync.dma_start(out=x_raw[1][:], in_=x_view[:, 2:4, :])
+        nc.gpsimd.memset(w_sc[:].rearrange("p g n -> p (g n)").bitcast(I32), 0)
+        for q in (2, 3):
+            nc.sync.dma_start(out=x_raw[q][:], in_=x_view[:, 2 * q : 2 * q + 2, :])
+        for r in range(4):
+            nc.sync.dma_start(
+                out=w_sc[32 * r : 32 * r + 4, :, :].bitcast(I32),
+                in_=W_scales[:, 4 * r : 4 * r + 4, :].rearrange("g r n -> r g n").bitcast(I32),
+            )
+        for g in (0, 2):
+            nc.sync.dma_start(
+                out=w_sb[:, g : g + 2, :].bitcast(I32),
+                in_=W_words[g : g + 2].rearrange("g p w -> p g w").bitcast(I32),
+            )
+        nc.sync.dma_start(out=row_bf[:], in_=row.rearrange("(p i) -> p i", i=NT))
+
+        warm = keep.tile([P, 512], BF16, name="warm")
+        warm_out = keep.tile([P, 1], F32, name="warm_out")
+        nc.vector.memset(warm[:], 0.0)
+        nc.scalar.activation(out=warm_out[:], in_=warm[:, 0:1], func=EXP)
+        warm_bank = psum.tile([P, 512], F32, tag="bank", name="warm_bank")
+
+        def spin(n):
+            for k in range(n):
+                nc.tensor.matmul(warm_bank[:], lhsT=warm[:, 0:P], rhs=warm[:], start=True, stop=True)
+
+        spin(4)
+
+        x_bf, x_tr, x_grp, c_tr, c_grp = {}, {}, {}, {}, {}
+        z_bank, e_tile, h_grp, y_bank = {}, {}, {}, {}
+
+        def x_widen(q, i):
+            xb = stage.tile([P, K], BF16, tag="xb", name="xb", bufs=4)
+            x_bf[q, i] = xb
+            for b in range(8):
+                nc.vector.tensor_scalar(
+                    out=xb[:, P * b : P * b + P],
+                    in0=x_raw[q][:, i, P * b : P * b + P].bitcast(F8),
+                    scalar1=x_sc[:, 2 * q + i, b : b + 1],
+                    scalar2=None,
+                    op0=MULT,
+                )
+
+        def x_turn(q, i):
+            tr = psum.tile([P, 2, 2, P], F32, tag="bank", name="x_bank")
+            x_tr[q, i] = tr
+            words = x_bf.pop((q, i))[:].bitcast(F32)
+            for g in range(2):
+                for u in range(2):
+                    nc.tensor.transpose(tr[:, g, u, :], words[:, 256 * g + u : 256 * (g + 1) : 2], ident[:])
+
+        def x_out(q, i, engine):
+            if i == 0:
+                x_grp[q] = stage.tile([P, 2, QT, 4], BF16, tag="x_grp", name="x_grp_t", align_bytes=64)
+            dst = x_grp[q][:, :, P * i : P * i + P, :].bitcast(F32)
+            src = x_tr.pop((q, i))[:].rearrange("p g u m -> p g m u")
+            if engine == "vector":
+                nc.vector.tensor_copy(out=dst, in_=src)
+            else:
+                nc.scalar.copy(out=dst, in_=src)
+
+        def x_quant(q):
+            grp = x_grp.pop(q)
+            for g in range(2):
+                nc.vector.quantize_mx(
+                    out=x_codes[q][:, g, :].bitcast(FP8X4),
+                    scales=x_planes[q][:, g, :],
+                    in_=grp[:, g, :, :].rearrange("p m j -> p (m j)"),
+                )
+
+        def c_turn(c):
+            tr = psum.tile([P, 2, 2, P], F32, tag="bank", name="c_bank")
+            c_tr[c] = tr
+            words = c_raw[c // 4][:, c % 4, :].bitcast(F32)
+            for g in range(2):
+                for u in range(2):
+                    nc.tensor.transpose(tr[:, g, u, :], words[:, 256 * g + u : 256 * (g + 1) : 2], ident[:])
+
+        def c_out(c):
+            grp = stage.tile([P, 2, P, 4], BF16, tag="c_grp", name="c_grp_t", align_bytes=64, bufs=4)
+            c_grp[c] = grp
+            nc.scalar.copy(out=grp[:].bitcast(F32), in_=c_tr.pop(c)[:].rearrange("p g u m -> p g m u"))
+
+        def c_quant(c):
+            nc.vector.quantize_mx(
+                out=c_codes[c][:].rearrange("p g m -> p (g m)").bitcast(FP8X4),
+                scales=c_planes[c][:].rearrange("p g m -> p (g m)"),
+                in_=c_grp.pop(c)[:].rearrange("p g m j -> p (g m j)"),
+            )
+
+        def first_product(g, q):
+            for a in range(2):
+                z = psum.tile([P, 2, QT], F32, tag="bank", name="z_bank_t")
+                z_bank[g, q, a] = z
+                for b in range(2):
+                    c = 4 * g + 2 * a + b
+                    for h in range(2):
+                        nc.tensor.matmul_mx(
+                            out=z[:, b, :],
+                            lhsT=c_codes[c][:, h, :].bitcast(FP8X4),
+                            lhsT_scale=c_planes[c][:, h, :],
+                            rhs=x_codes[q][:, h, :].bitcast(FP8X4),
+                            rhs_scale=x_planes[q][:, h, :],
+                            start=(h == 0),
+                            stop=(h == 1),
+                        )
+
+        def exponentials(g, q):
+            e = stage.tile([P, 2, QT, 2], F32, tag="e", name="e_t")
+            e_tile[g, q] = e
+            for a in range(2):
+                nc.scalar.activation(out=e[:, a, :, :], in_=z_bank.pop((g, q, a))[:].rearrange("p b t -> p t b"), func=EXP)
+
+        def times_amp(g, q):
+            hg = stage.tile([P, QT, 4], BF16, tag="h_grp", name="h_grp_t", align_bytes=64)
+            h_grp[g, q] = hg
+            e = e_tile.pop((g, q))
+            for t0 in range(0, QT, P):
+                nc.vector.tensor_tensor(
+                    out=hg[:, t0 : t0 + P, :].rearrange("p t (a b) -> p t a b", b=2),
+                    in0=e[:, :, t0 : t0 + P, :].rearrange("p a t b -> p t a b"),
+                    in1=amp_sb[:, g, :].rearrange("p (a b) -> p a b", b=2).unsqueeze(1).to_broadcast([P, P, 2, 2]),
+                    op=MULT,
+                )
+
+        def h_quant(g, q):
+            hg = h_grp.pop((g, q))
+            for t0 in range(0, QT, P):
+                nc.vector.quantize_mx(
+                    out=h_codes[q][g][:, t0 : t0 + P].bitcast(FP8X4),
+                    scales=h_planes[q][g][:, t0 : t0 + P],
+                    in_=hg[:, t0 : t0 + P, :].rearrange("p t j -> p (t j)"),
+                )
+
+        def second_product(q, u, gs):
+            i, dh = u // 2, u % 2
+            if gs[0] == 0:
+                y_bank[q, u] = psum.tile([P, 512], F32, tag="bank", name="y_bank_t")
+            for g in gs:
+                nc.tensor.matmul_mx(
+                    out=y_bank[q, u][:],
+                    lhsT=h_codes[q][g][:, P * i : P * i + P].bitcast(FP8X4),
+                    lhsT_scale=h_planes[q][g][:, P * i : P * i + P],
+                    rhs=w_sb[:, g, 1024 * dh : 1024 * dh + 1024].bitcast(FP4X4),
+                    rhs_scale=w_sc[:, g, 512 * dh : 512 * dh + 512],
+                    start=(g == 0),
+                    stop=(g == NG - 1),
+                )
+
+        out_view = out.rearrange("(p i) d -> p i d", i=NT)
+
+        def store(q, u, engine):
+            i, dh = 2 * q + u // 2, u % 2
+            y = stage.tile([P, 512], F32, tag="y", name="y_t", bufs=4)
+            if engine == "vector":
+                nc.vector.tensor_scalar(out=y[:], in0=y_bank.pop((q, u))[:], scalar1=row_sb[:, i : i + 1], scalar2=None, op0=MULT)
+            else:
+                nc.scalar.activation(out=y[:], in_=y_bank.pop((q, u))[:], func=COPY, scale=row_sb[:, i : i + 1])
+            nc.sync.dma_start(out=out_view[:, i, 512 * dh : 512 * dh + 512], in_=y[:])
+
+        x_widen(0, 0)
+        x_widen(0, 1)
+        c_turn(0)
+        c_out(0)
+        spin(2)
+        c_turn(1)
+        c_out(1)
+        spin(1)
+        x_turn(0, 0)
+        x_out(0, 0, "scalar")
+        c_turn(2)
+        c_out(2)
+        x_turn(0, 1)
+        x_out(0, 1, "vector")
+        c_turn(3)
+        c_out(3)
+        spin(1)
+        c_quant(0)
+        c_quant(1)
+        x_quant(0)
+        c_quant(2)
+        c_quant(3)
+
+        for c in range(4, 8):
+            c_turn(c)
+            c_out(c)
+            c_quant(c)
+            if c == 5:
+                spin(1)
+        first_product(0, 0)
+        exponentials(0, 0)
+        x_widen(1, 0)
+        x_widen(1, 1)
+        for c in range(8, 12):
+            c_turn(c)
+            c_out(c)
+            c_quant(c)
+            if c == 8:
+                times_amp(0, 0)
+            if c == 9:
+                h_quant(0, 0)
+        first_product(1, 0)
+        exponentials(1, 0)
+        x_turn(1, 0)
+        x_turn(1, 1)
+        spin(1)
+        x_out(1, 0, "scalar")
+        x_out(1, 1, "scalar")
+        for c in range(12, 16):
+            c_turn(c)
+            c_out(c)
+            c_quant(c)
+            if c == 12:
+                times_amp(1, 0)
+            if c == 12+1:
+                h_quant(1, 0)
+            if c == 14:
+                x_quant(1)
+        nc.vector.tensor_copy(out=row_sb[:], in_=row_bf[:])
+
+        beside = {2: [(2, 0), (2, 1)], 3: [(3, 0)], 4: [(3, 1)]}
+        finished, fresh = [], []
+        units = [(q, u) for q in range(1, NQ) for u in range(4)]
+        for s in range(2, NQ * NG + 1):
+            q, g = s // NG, s % NG
+            if s < NQ * NG:
+                first_product(g, q)
+                exponentials(g, q)
+            if s == 6:
+                for n in (2, 3):
+                    for i in range(2):
+                        x_turn(n, i)
+                for n in (2, 3):
+                    for i in range(2):
+                        x_out(n, i, "scalar")
+            if s > 2:
+                times_amp((s - 1) % NG, (s - 1) // NG)
+                for n in beside.get(s - 1, []):
+                    x_widen(*n)
+                if s == 6:
+                    x_quant(2)
+                if s == 6 + 1:
+                    x_quant(3)
+                h_quant((s - 1) % NG, (s - 1) // NG)
+            g = {2: 0, 4: 1, 5: 2, 7: 3}.get(s)
+            if g is not None:
+                for u in range(4):
+                    second_product(0, u, [g])
+                if g == NG - 1:
+                    fresh = [(0, u) for u in range(4)]
+            elif s >= 9 and s < NQ * NG:
+                unit = units.pop(0)
+                second_product(*unit, range(NG))
+                fresh = [unit]
+            for unit in finished[:2]:
+                store(*unit, "scalar")
+            finished = finished[2:] + fresh
+            fresh = []
+        last = NQ - 1
+        for unit in finished:
+            store(*unit, "scalar")
+        while len(units) > 1:
+            unit = units.pop(0)
+            second_product(*unit, range(NG))
+            store(*unit, "scalar" if unit[1] % 2 == 0 else "vector")
+        second_product(last, 3, range(NG))
+        i = NT - 1
+        y = stage.tile([P, 512], F32, tag="y", name="y_t", bufs=4)
+        y2 = stage.tile([P, 256], F32, tag="y2", name="y2_t", bufs=1)
+        bank = y_bank.pop((last, 3))
+        nc.scalar.activation(out=y[:, 0:256], in_=bank[:, 0:256], func=COPY, scale=row_sb[:, i : i + 1])
+        nc.vector.tensor_scalar(out=y2[:], in0=bank[:, 256:512], scalar1=row_sb[:, i : i + 1], scalar2=None, op0=MULT)
+        nc.sync.dma_start(out=out_view[:, i, 512:768], in_=y[:, 0:256])
+        nc.sync.dma_start(out=out_view[:, i, 768:1024], in_=y2[:])

@@ -80,9 +80,7 @@ def tile_rbf_kernel_readout_d4_kernel(tc, X_bytes, X_scale, C, amp, row, W_words
         nc.sync.dma_start(out=row_bf[:], in_=row.rearrange("(p i) -> p i", i=NT))
 
         warm = keep.tile([P, 512], BF16, name="warm")
-        warm_out = keep.tile([P, 1], F32, name="warm_out")
         nc.vector.memset(warm[:], 0.0)
-        nc.scalar.activation(out=warm_out[:], in_=warm[:, 0:1], func=EXP)
         warm_bank = psum.tile([P, 512], F32, tag="bank", name="warm_bank")
 
         def spin(n):

@@ -87,7 +87,7 @@ def tile_rbf_kernel_readout_d4_kernel(tc, X_bytes, X_scale, C, amp, row, W_words
             for k in range(n):
                 nc.tensor.matmul(warm_bank[:], lhsT=warm[:, 0:P], rhs=warm[:], start=True, stop=True)
 
-        spin(4)
+        spin(3)
 
         x_bf, x_tr, x_grp, c_tr, c_grp = {}, {}, {}, {}, {}
         z_bank, e_tile, h_grp, y_bank = {}, {}, {}, {}
@@ -140,7 +140,7 @@ def tile_rbf_kernel_readout_d4_kernel(tc, X_bytes, X_scale, C, amp, row, W_words
                     nc.tensor.transpose(tr[:, g, u, :], words[:, 256 * g + u : 256 * (g + 1) : 2], ident[:])
 
         def c_out(c):
-            grp = stage.tile([P, 2, P, 4], BF16, tag="c_grp", name="c_grp_t", align_bytes=64, bufs=4)
+            grp = stage.tile([P, 2, P, 4], BF16, tag="c_grp", name="c_grp_t", align_bytes=64, bufs=8)
             c_grp[c] = grp
             nc.scalar.copy(out=grp[:].bitcast(F32), in_=c_tr.pop(c)[:].rearrange("p g u m -> p g m u"))
 
@@ -169,7 +169,7 @@ def tile_rbf_kernel_readout_d4_kernel(tc, X_bytes, X_scale, C, amp, row, W_words
                         )
 
         def exponentials(g, q):
-            e = stage.tile([P, 2, QT, 2], F32, tag="e", name="e_t")
+            e = stage.tile([P, 2, QT, 2], F32, tag="e", name="e_t", bufs=5)
             e_tile[g, q] = e
             for a in range(2):
                 nc.scalar.activation(out=e[:, a, :, :], in_=z_bank.pop((g, q, a))[:].rearrange("p b t -> p t b"), func=EXP)
@@ -214,7 +214,7 @@ def tile_rbf_kernel_readout_d4_kernel(tc, X_bytes, X_scale, C, amp, row, W_words
 
         def store(q, u, engine):
             i, dh = 2 * q + u // 2, u % 2
-            y = stage.tile([P, 512], F32, tag="y", name="y_t", bufs=4)
+            y = stage.tile([P, 512], F32, tag="y", name="y_t", bufs=2 * NT)
             if engine == "vector":
                 nc.vector.tensor_scalar(out=y[:], in0=y_bank.pop((q, u))[:], scalar1=row_sb[:, i : i + 1], scalar2=None, op0=MULT)
             else:
@@ -328,7 +328,7 @@ def tile_rbf_kernel_readout_d4_kernel(tc, X_bytes, X_scale, C, amp, row, W_words
             store(*unit, "scalar" if unit[1] % 2 == 0 else "vector")
         second_product(last, 3, range(NG))
         i = NT - 1
-        y = stage.tile([P, 512], F32, tag="y", name="y_t", bufs=4)
+        y = stage.tile([P, 512], F32, tag="y", name="y_t", bufs=2 * NT)
         y2 = stage.tile([P, 256], F32, tag="y2", name="y2_t", bufs=1)
         bank = y_bank.pop((last, 3))
         nc.scalar.activation(out=y[:, 0:256], in_=bank[:, 0:256], func=COPY, scale=row_sb[:, i : i + 1])

@@ -65,8 +65,6 @@ def tile_rbf_kernel_readout_d4_kernel(tc, X_bytes, X_scale, C, amp, row, W_words
             if g == 1:
                 nc.sync.dma_start(out=x_raw[1][:], in_=x_view[:, 2:4, :])
         nc.gpsimd.memset(w_sc[:].rearrange("p g n -> p (g n)").bitcast(I32), 0)
-        for q in (2, 3):
-            nc.sync.dma_start(out=x_raw[q][:], in_=x_view[:, 2 * q : 2 * q + 2, :])
         for r in range(4):
             nc.sync.dma_start(
                 out=w_sc[32 * r : 32 * r + 4, :, :].bitcast(I32),
@@ -77,6 +75,9 @@ def tile_rbf_kernel_readout_d4_kernel(tc, X_bytes, X_scale, C, amp, row, W_words
                 out=w_sb[:, g : g + 2, :].bitcast(I32),
                 in_=W_words[g : g + 2].rearrange("g p w -> p g w").bitcast(I32),
             )
+            if g == 0:
+                for q in (2, 3):
+                    nc.sync.dma_start(out=x_raw[q][:], in_=x_view[:, 2 * q : 2 * q + 2, :])
         nc.sync.dma_start(out=row_bf[:], in_=row.rearrange("(p i) -> p i", i=NT))
 
         warm = keep.tile([P, 512], BF16, name="warm")
@@ -279,7 +280,6 @@ def tile_rbf_kernel_readout_d4_kernel(tc, X_bytes, X_scale, C, amp, row, W_words
                 h_quant(1, 0)
             if c == 14:
                 x_quant(1)
-        nc.vector.tensor_copy(out=row_sb[:], in_=row_bf[:])
 
         beside = {2: [(2, 0), (2, 1)], 3: [(3, 0)], 4: [(3, 1)]}
         finished, fresh = [], []
@@ -304,6 +304,7 @@ def tile_rbf_kernel_readout_d4_kernel(tc, X_bytes, X_scale, C, amp, row, W_words
                     x_quant(2)
                 if s == 6 + 1:
                     x_quant(3)
+                    nc.vector.tensor_copy(out=row_sb[:], in_=row_bf[:])
                 h_quant((s - 1) % NG, (s - 1) // NG)
             g = {2: 0, 4: 1, 5: 2, 7: 3}.get(s)
             if g is not None:
@@ -332,6 +333,6 @@ def tile_rbf_kernel_readout_d4_kernel(tc, X_bytes, X_scale, C, amp, row, W_words
         y2 = stage.tile([P, 256], F32, tag="y2", name="y2_t", bufs=1)
         bank = y_bank.pop((last, 3))
         nc.scalar.activation(out=y[:, 0:256], in_=bank[:, 0:256], func=COPY, scale=row_sb[:, i : i + 1])
-        nc.vector.tensor_scalar(out=y2[:], in0=bank[:, 256:512], scalar1=row_sb[:, i : i + 1], scalar2=None, op0=MULT)
         nc.sync.dma_start(out=out_view[:, i, 512:768], in_=y[:, 0:256])
+        nc.scalar.activation(out=y2[:], in_=bank[:, 256:512], func=COPY, scale=row_sb[:, i : i + 1])
         nc.sync.dma_start(out=out_view[:, i, 768:1024], in_=y2[:])

@@ -34,13 +34,15 @@ def tile_rbf_kernel_readout_d4_kernel(tc, X_bytes, X_scale, C, amp, row, W_words
         ctx.enter_context(tc.manual_schedule())
 
         ident = keep.tile([P, P], F32, name="ident")
-        x_raw = [keep.tile([P, 2, K], U8, name="x_raw%d" % q) for q in range(NQ)]
+        x_raw = [keep.tile([P, K], U8, name="x_raw%d" % i) for i in range(2)]
+        x_raw_late = [keep.tile([P, 2, K], U8, name="x_raw_late%d" % q) for q in range(1, NQ)]
         x_sc = keep.tile([P, NT, 8], F32, name="x_sc")
-        c_raw = [keep.tile([P, 4, K], BF16, name="c_raw%d" % g) for g in range(NG)]
+        c_first = [keep.tile([P, K], BF16, name="c_first%d" % t) for t in range(4)]
+        c_pairs = [keep.tile([P, 2, K], BF16, name="c_pairs%d" % n) for n in range(2, 2 * NG)]
         amp_sb = keep.tile([P, NG, 4], BF16, name="amp_sb")
         row_bf = keep.tile([P, NT], BF16, name="row_bf")
         row_sb = keep.tile([P, NT], F32, name="row_sb")
-        w_sb = keep.tile([P, NG, 2 * D], U8, name="w_sb", align_bytes=64)
+        w_sb = [keep.tile([P, 2 * D], U8, name="w_sb%d" % g, align_bytes=64) for g in range(NG)]
         w_sc = keep.tile([P, NG, D], U8, name="w_sc", align_bytes=64)
         x_codes = [keep.tile([P, 2, QT], U32, name="x_codes%d" % q, align_bytes=64) for q in range(NQ)]
         x_planes = [keep.tile([P, 2, QT], U8, name="x_planes%d" % q, align_bytes=64) for q in range(NQ)]
@@ -50,289 +52,325 @@ def tile_rbf_kernel_readout_d4_kernel(tc, X_bytes, X_scale, C, amp, row, W_words
         h_planes = [[keep.tile([P, QT], U8, name="h_planes%d_%d" % (q, g), align_bytes=64) for g in range(NG)] for q in range(NQ)]
 
         make_identity(nc, ident[:])
+        warm = keep.tile([P, 512], BF16, name="warm")
+        nc.vector.memset(warm[:], 0.0)
+        nc.vector.memset(w_sc[:].rearrange("p g n -> p (g n)").bitcast(I32), 0)
 
         x_view = X_bytes.rearrange("(p i) k -> p i k", i=NT)
         c_view = C.rearrange("(g m t) k -> g m t k", g=NG, t=4)
-        nc.sync.dma_start(out=c_raw[0][:, 0:1, :], in_=c_view[0][:, 0:1, :])
+
+        def x_bytes(i):
+            return x_raw[i][:] if i < 2 else x_raw_late[i // 2 - 1][:, i % 2, :]
+
+        def c_rows(c):
+            return c_first[c][:] if c < 4 else c_pairs[c // 2 - 2][:, c % 2, :]
+
+        def load_c_pair(n):
+            nc.sync.dma_start(out=c_pairs[n - 2][:], in_=c_view[n // 2][:, 2 * (n % 2) : 2 * (n % 2) + 2, :])
+
+        def load_x_quarter(q):
+            nc.sync.dma_start(out=x_raw_late[q - 1][:], in_=x_view[:, 2 * q : 2 * q + 2, :])
+
+        def load_w(g):
+            nc.sync.dma_start(out=w_sb[g][:].bitcast(I32), in_=W_words[g].bitcast(I32))
+
+        def load_w_scales():
+            for r in range(4):
+                nc.sync.dma_start(
+                    out=w_sc[32 * r : 32 * r + 4, :, :].bitcast(I32),
+                    in_=W_scales[:, 4 * r : 4 * r + 4, :].rearrange("g r n -> r g n").bitcast(I32),
+                )
+
+        nc.sync.dma_start(out=c_first[0][:], in_=c_view[0][:, 0, :])
         nc.sync.dma_start(out=x_sc[:], in_=X_scale.rearrange("(p i) b -> p i b", i=NT))
-        nc.sync.dma_start(out=x_raw[0][:], in_=x_view[:, 0:2, :])
-        for t in range(1, 4):
-            nc.sync.dma_start(out=c_raw[0][:, t : t + 1, :], in_=c_view[0][:, t : t + 1, :])
+        nc.sync.dma_start(out=x_raw[0][:], in_=x_view[:, 0, :])
+        nc.sync.dma_start(out=c_first[1][:], in_=c_view[0][:, 1, :])
+        nc.sync.dma_start(out=x_raw[1][:], in_=x_view[:, 1, :])
+        for t in (2, 3):
+            nc.sync.dma_start(out=c_first[t][:], in_=c_view[0][:, t, :])
+        load_c_pair(2)
+        load_x_quarter(1)
+        load_c_pair(3)
         nc.sync.dma_start(out=amp_sb[:], in_=amp.rearrange("(g m t) -> m g t", g=NG, t=4))
+        load_c_pair(4)
+        load_c_pair(5)
+        load_x_quarter(2)
+        load_c_pair(6)
+        load_w_scales()
+        load_w(0)
+        load_c_pair(7)
+        load_x_quarter(3)
         for g in range(1, NG):
-            for t in (0, 2):
-                nc.sync.dma_start(out=c_raw[g][:, t : t + 2, :], in_=c_view[g][:, t : t + 2, :])
-            if g == 1:
-                nc.sync.dma_start(out=x_raw[1][:], in_=x_view[:, 2:4, :])
-        nc.gpsimd.memset(w_sc[:].rearrange("p g n -> p (g n)").bitcast(I32), 0)
-        for r in range(4):
-            nc.sync.dma_start(
-                out=w_sc[32 * r : 32 * r + 4, :, :].bitcast(I32),
-                in_=W_scales[:, 4 * r : 4 * r + 4, :].rearrange("g r n -> r g n").bitcast(I32),
-            )
-        for g in (0, 2):
-            nc.sync.dma_start(
-                out=w_sb[:, g : g + 2, :].bitcast(I32),
-                in_=W_words[g : g + 2].rearrange("g p w -> p g w").bitcast(I32),
-            )
-            if g == 0:
-                for q in (2, 3):
-                    nc.sync.dma_start(out=x_raw[q][:], in_=x_view[:, 2 * q : 2 * q + 2, :])
+            load_w(g)
         nc.sync.dma_start(out=row_bf[:], in_=row.rearrange("(p i) -> p i", i=NT))
-
-        warm = keep.tile([P, 512], BF16, name="warm")
-        nc.vector.memset(warm[:], 0.0)
-        warm_bank = psum.tile([P, 512], F32, tag="bank", name="warm_bank")
-
-        def spin(n):
-            for k in range(n):
-                nc.tensor.matmul(warm_bank[:], lhsT=warm[:, 0:P], rhs=warm[:], start=True, stop=True)
-
-        spin(3)
 
         x_bf, x_tr, x_grp, c_tr, c_grp = {}, {}, {}, {}, {}
         z_bank, e_tile, h_grp, y_bank = {}, {}, {}, {}
 
-        def x_widen(q, i):
-            xb = stage.tile([P, K], BF16, tag="xb", name="xb", bufs=4)
-            x_bf[q, i] = xb
-            for b in range(8):
-                nc.vector.tensor_scalar(
-                    out=xb[:, P * b : P * b + P],
-                    in0=x_raw[q][:, i, P * b : P * b + P].bitcast(F8),
-                    scalar1=x_sc[:, 2 * q + i, b : b + 1],
-                    scalar2=None,
-                    op0=MULT,
-                )
+        def spin():
+            bank = psum.tile([P, 512], F32, tag="bank", name="warm_bank")
+            nc.tensor.matmul(bank[:], lhsT=warm[:, 0:P], rhs=warm[:], start=True, stop=True)
 
-        def x_turn(q, i):
-            tr = psum.tile([P, 2, 2, P], F32, tag="bank", name="x_bank")
-            x_tr[q, i] = tr
-            words = x_bf.pop((q, i))[:].bitcast(F32)
-            for g in range(2):
-                for u in range(2):
-                    nc.tensor.transpose(tr[:, g, u, :], words[:, 256 * g + u : 256 * (g + 1) : 2], ident[:])
-
-        def x_out(q, i, engine):
-            if i == 0:
-                x_grp[q] = stage.tile([P, 2, QT, 4], BF16, tag="x_grp", name="x_grp_t", align_bytes=64)
-            dst = x_grp[q][:, :, P * i : P * i + P, :].bitcast(F32)
-            src = x_tr.pop((q, i))[:].rearrange("p g u m -> p g m u")
+        def copy_out(engine, dst, src):
             if engine == "vector":
                 nc.vector.tensor_copy(out=dst, in_=src)
             else:
                 nc.scalar.copy(out=dst, in_=src)
 
-        def x_quant(q):
-            grp = x_grp.pop(q)
-            for g in range(2):
+        def turn(words):
+            tr = psum.tile([P, 2, 2, P], F32, tag="bank", name="turn_bank")
+            for h in range(2):
+                for u in range(2):
+                    nc.tensor.transpose(tr[:, h, u, :], words[:, 256 * h + u : 256 * (h + 1) : 2], ident[:])
+            return tr
+
+        def x_widen(i):
+            xb = stage.tile([P, K], BF16, tag="xb", name="xb", bufs=6)
+            x_bf[i] = xb
+            for b in range(8):
+                nc.vector.tensor_scalar(
+                    out=xb[:, P * b : P * b + P],
+                    in0=x_bytes(i)[:, P * b : P * b + P].bitcast(F8),
+                    scalar1=x_sc[:, i, b : b + 1],
+                    scalar2=None,
+                    op0=MULT,
+                )
+
+        def x_turn(i):
+            x_tr[i] = turn(x_bf.pop(i)[:].bitcast(F32))
+
+        def x_out(i, engine):
+            grp = stage.tile([P, 2, P, 4], BF16, tag="grp", name="x_grp_t", align_bytes=64, bufs=8)
+            x_grp[i] = grp
+            copy_out(engine, grp[:].bitcast(F32), x_tr.pop(i)[:].rearrange("p h u m -> p h m u"))
+
+        def x_quant(i):
+            grp = x_grp.pop(i)
+            cols = slice(P * (i % 2), P * (i % 2) + P)
+            for h in range(2):
                 nc.vector.quantize_mx(
-                    out=x_codes[q][:, g, :].bitcast(FP8X4),
-                    scales=x_planes[q][:, g, :],
-                    in_=grp[:, g, :, :].rearrange("p m j -> p (m j)"),
+                    out=x_codes[i // 2][:, h, cols].bitcast(FP8X4),
+                    scales=x_planes[i // 2][:, h, cols],
+                    in_=grp[:, h, :, :].rearrange("p m j -> p (m j)"),
                 )
 
         def c_turn(c):
-            tr = psum.tile([P, 2, 2, P], F32, tag="bank", name="c_bank")
-            c_tr[c] = tr
-            words = c_raw[c // 4][:, c % 4, :].bitcast(F32)
-            for g in range(2):
-                for u in range(2):
-                    nc.tensor.transpose(tr[:, g, u, :], words[:, 256 * g + u : 256 * (g + 1) : 2], ident[:])
+            c_tr[c] = turn(c_rows(c).bitcast(F32))
 
-        def c_out(c):
-            grp = stage.tile([P, 2, P, 4], BF16, tag="c_grp", name="c_grp_t", align_bytes=64, bufs=8)
+        def c_out(c, engine="scalar"):
+            grp = stage.tile([P, 2, P, 4], BF16, tag="grp", name="c_grp_t", align_bytes=64, bufs=8)
             c_grp[c] = grp
-            nc.scalar.copy(out=grp[:].bitcast(F32), in_=c_tr.pop(c)[:].rearrange("p g u m -> p g m u"))
+            copy_out(engine, grp[:].bitcast(F32), c_tr.pop(c)[:].rearrange("p h u m -> p h m u"))
 
         def c_quant(c):
             nc.vector.quantize_mx(
-                out=c_codes[c][:].rearrange("p g m -> p (g m)").bitcast(FP8X4),
-                scales=c_planes[c][:].rearrange("p g m -> p (g m)"),
-                in_=c_grp.pop(c)[:].rearrange("p g m j -> p (g m j)"),
+                out=c_codes[c][:].rearrange("p h m -> p (h m)").bitcast(FP8X4),
+                scales=c_planes[c][:].rearrange("p h m -> p (h m)"),
+                in_=c_grp.pop(c)[:].rearrange("p h m j -> p (h m j)"),
             )
 
-        def first_product(g, q):
-            for a in range(2):
-                z = psum.tile([P, 2, QT], F32, tag="bank", name="z_bank_t")
-                z_bank[g, q, a] = z
-                for b in range(2):
-                    c = 4 * g + 2 * a + b
-                    for h in range(2):
-                        nc.tensor.matmul_mx(
-                            out=z[:, b, :],
-                            lhsT=c_codes[c][:, h, :].bitcast(FP8X4),
-                            lhsT_scale=c_planes[c][:, h, :],
-                            rhs=x_codes[q][:, h, :].bitcast(FP8X4),
-                            rhs_scale=x_planes[q][:, h, :],
-                            start=(h == 0),
-                            stop=(h == 1),
-                        )
+        def first_half(q, g, a):
+            z = psum.tile([P, 2, QT], F32, tag="bank", name="z_bank_t")
+            z_bank[q, g, a] = z
+            for b in range(2):
+                c = 4 * g + 2 * a + b
+                for h in range(2):
+                    nc.tensor.matmul_mx(
+                        out=z[:, b, :],
+                        lhsT=c_codes[c][:, h, :].bitcast(FP8X4),
+                        lhsT_scale=c_planes[c][:, h, :],
+                        rhs=x_codes[q][:, h, :].bitcast(FP8X4),
+                        rhs_scale=x_planes[q][:, h, :],
+                        start=(h == 0),
+                        stop=(h == 1),
+                    )
 
-        def exponentials(g, q):
-            e = stage.tile([P, 2, QT, 2], F32, tag="e", name="e_t", bufs=5)
-            e_tile[g, q] = e
-            for a in range(2):
-                nc.scalar.activation(out=e[:, a, :, :], in_=z_bank.pop((g, q, a))[:].rearrange("p b t -> p t b"), func=EXP)
+        def exponential(q, g, a):
+            if a == 0:
+                e_tile[q, g] = stage.tile([P, 2, QT, 2], F32, tag="e", name="e_t", bufs=7)
+            nc.scalar.activation(out=e_tile[q, g][:, a, :, :], in_=z_bank.pop((q, g, a))[:].rearrange("p b t -> p t b"), func=EXP)
 
-        def times_amp(g, q):
+        def times_amp(q, g, parts=1):
             hg = stage.tile([P, QT, 4], BF16, tag="h_grp", name="h_grp_t", align_bytes=64)
-            h_grp[g, q] = hg
-            e = e_tile.pop((g, q))
-            for t0 in range(0, QT, P):
+            h_grp[q, g] = hg
+            e = e_tile.pop((q, g))
+            n = QT // parts
+            for t0 in range(0, QT, n):
                 nc.vector.tensor_tensor(
-                    out=hg[:, t0 : t0 + P, :].rearrange("p t (a b) -> p t a b", b=2),
-                    in0=e[:, :, t0 : t0 + P, :].rearrange("p a t b -> p t a b"),
-                    in1=amp_sb[:, g, :].rearrange("p (a b) -> p a b", b=2).unsqueeze(1).to_broadcast([P, P, 2, 2]),
+                    out=hg[:, t0 : t0 + n, :].rearrange("p t (a b) -> p t a b", b=2),
+                    in0=e[:, :, t0 : t0 + n, :].rearrange("p a t b -> p t a b"),
+                    in1=amp_sb[:, g, :].rearrange("p (a b) -> p a b", b=2).unsqueeze(1).to_broadcast([P, n, 2, 2]),
                     op=MULT,
                 )
 
-        def h_quant(g, q):
-            hg = h_grp.pop((g, q))
-            for t0 in range(0, QT, P):
+        def h_quant(q, g, parts=1):
+            hg = h_grp.pop((q, g))
+            n = QT // parts
+            for t0 in range(0, QT, n):
                 nc.vector.quantize_mx(
-                    out=h_codes[q][g][:, t0 : t0 + P].bitcast(FP8X4),
-                    scales=h_planes[q][g][:, t0 : t0 + P],
-                    in_=hg[:, t0 : t0 + P, :].rearrange("p t j -> p (t j)"),
+                    out=h_codes[q][g][:, t0 : t0 + n].bitcast(FP8X4),
+                    scales=h_planes[q][g][:, t0 : t0 + n],
+                    in_=hg[:, t0 : t0 + n, :].rearrange("p t j -> p (t j)"),
                 )
 
+        def second_pass(bank, q, i, g, d0, width):
+            nc.tensor.matmul_mx(
+                out=bank,
+                lhsT=h_codes[q][g][:, P * i : P * i + P].bitcast(FP8X4),
+                lhsT_scale=h_planes[q][g][:, P * i : P * i + P],
+                rhs=w_sb[g][:, 2 * d0 : 2 * (d0 + width)].bitcast(FP4X4),
+                rhs_scale=w_sc[:, g, d0 : d0 + width],
+                start=(g == 0),
+                stop=(g == NG - 1),
+            )
+
         def second_product(q, u, gs):
-            i, dh = u // 2, u % 2
             if gs[0] == 0:
                 y_bank[q, u] = psum.tile([P, 512], F32, tag="bank", name="y_bank_t")
             for g in gs:
-                nc.tensor.matmul_mx(
-                    out=y_bank[q, u][:],
-                    lhsT=h_codes[q][g][:, P * i : P * i + P].bitcast(FP8X4),
-                    lhsT_scale=h_planes[q][g][:, P * i : P * i + P],
-                    rhs=w_sb[:, g, 1024 * dh : 1024 * dh + 1024].bitcast(FP4X4),
-                    rhs_scale=w_sc[:, g, 512 * dh : 512 * dh + 512],
-                    start=(g == 0),
-                    stop=(g == NG - 1),
-                )
+                second_pass(y_bank[q, u][:], q, u // 2, g, 512 * (u % 2), 512)
 
         out_view = out.rearrange("(p i) d -> p i d", i=NT)
 
-        def store(q, u, engine):
-            i, dh = 2 * q + u // 2, u % 2
-            y = stage.tile([P, 512], F32, tag="y", name="y_t", bufs=2 * NT)
+        def scale_and_store(bank, i, d0, width, engine):
+            y = stage.tile([P, 512], F32, tag="y", name="y_t", bufs=8)
             if engine == "vector":
-                nc.vector.tensor_scalar(out=y[:], in0=y_bank.pop((q, u))[:], scalar1=row_sb[:, i : i + 1], scalar2=None, op0=MULT)
+                nc.vector.tensor_scalar(out=y[:, 0:width], in0=bank, scalar1=row_sb[:, i : i + 1], scalar2=None, op0=MULT)
             else:
-                nc.scalar.activation(out=y[:], in_=y_bank.pop((q, u))[:], func=COPY, scale=row_sb[:, i : i + 1])
-            nc.sync.dma_start(out=out_view[:, i, 512 * dh : 512 * dh + 512], in_=y[:])
+                nc.scalar.activation(out=y[:, 0:width], in_=bank, func=COPY, scale=row_sb[:, i : i + 1])
+            nc.sync.dma_start(out=out_view[:, i, d0 : d0 + width], in_=y[:, 0:width])
 
-        x_widen(0, 0)
-        x_widen(0, 1)
-        c_turn(0)
-        c_out(0)
-        spin(2)
-        c_turn(1)
-        c_out(1)
-        spin(1)
-        x_turn(0, 0)
-        x_out(0, 0, "scalar")
-        c_turn(2)
-        c_out(2)
-        x_turn(0, 1)
-        x_out(0, 1, "vector")
-        c_turn(3)
-        c_out(3)
-        spin(1)
+        def store(q, u, engine):
+            scale_and_store(y_bank.pop((q, u))[:], 2 * q + u // 2, 512 * (u % 2), 512, engine)
+
+        def first_product(q, g):
+            for a in range(2):
+                first_half(q, g, a)
+                exponential(q, g, a)
+
+        def c_tile(c):
+            c_turn(c)
+            c_out(c)
+
+        def x_tile(i):
+            x_turn(i)
+            x_out(i, "scalar")
+
+        for k in range(3):
+            spin()
+        x_widen(0)
+        x_widen(1)
+        c_tile(0)
+        spin()
+        c_tile(1)
+        x_tile(0)
         c_quant(0)
+        x_turn(1)
+        spin()
         c_quant(1)
+        x_out(1, "vector")
         x_quant(0)
+        x_quant(1)
+        for c in range(2, 6):
+            c_tile(c)
         c_quant(2)
         c_quant(3)
-
-        for c in range(4, 8):
-            c_turn(c)
-            c_out(c)
-            c_quant(c)
-            if c == 5:
-                spin(1)
         first_product(0, 0)
-        exponentials(0, 0)
-        x_widen(1, 0)
-        x_widen(1, 1)
-        for c in range(8, 12):
-            c_turn(c)
-            c_out(c)
-            c_quant(c)
-            if c == 8:
-                times_amp(0, 0)
-            if c == 9:
-                h_quant(0, 0)
-        first_product(1, 0)
-        exponentials(1, 0)
-        x_turn(1, 0)
-        x_turn(1, 1)
-        spin(1)
-        x_out(1, 0, "scalar")
-        x_out(1, 1, "scalar")
-        for c in range(12, 16):
-            c_turn(c)
-            c_out(c)
-            c_quant(c)
-            if c == 12:
-                times_amp(1, 0)
-            if c == 12+1:
-                h_quant(1, 0)
-            if c == 14:
-                x_quant(1)
+        x_widen(2)
+        c_quant(4)
+        c_quant(5)
 
-        beside = {2: [(2, 0), (2, 1)], 3: [(3, 0)], 4: [(3, 1)]}
-        finished, fresh = [], []
+        for c in range(6, 10):
+            c_tile(c)
+        x_widen(3)
+        c_quant(6)
+        c_quant(7)
+        first_product(0, 1)
+        times_amp(0, 0)
+        c_quant(8)
+        c_quant(9)
+        h_quant(0, 0)
+
+        for c in range(10, 14):
+            c_tile(c)
+        x_widen(4)
+        c_quant(10)
+        c_quant(11)
+        for u in range(4):
+            second_product(0, u, [0])
+        first_product(0, 2)
+        times_amp(0, 1)
+        c_quant(12)
+        c_quant(13)
+        h_quant(0, 1)
+
+        c_tile(14)
+        c_tile(15)
+        x_tile(2)
+        x_tile(3)
+        x_widen(5)
+        c_quant(14)
+        c_quant(15)
+        for u in range(4):
+            second_product(0, u, [1])
+        first_product(0, 3)
+        x_widen(6)
+        x_quant(2)
+        x_quant(3)
+        first_product(1, 0)
+        times_amp(0, 2)
+        x_widen(7)
+        h_quant(0, 2)
+
+        for i in range(4, 8):
+            x_tile(i)
+        for u in range(4):
+            second_product(0, u, [2])
+        times_amp(0, 3)
+        nc.vector.tensor_copy(out=row_sb[:], in_=row_bf[:])
+        h_quant(0, 3)
+        times_amp(1, 0)
+
+        steps = [(q, g) for q in range(1, NQ) for g in range(NG)]
         units = [(q, u) for q in range(1, NQ) for u in range(4)]
-        for s in range(2, NQ * NG + 1):
-            q, g = s // NG, s % NG
-            if s < NQ * NG:
-                first_product(g, q)
-                exponentials(g, q)
-            if s == 6:
-                for n in (2, 3):
-                    for i in range(2):
-                        x_turn(n, i)
-                for n in (2, 3):
-                    for i in range(2):
-                        x_out(n, i, "scalar")
-            if s > 2:
-                times_amp((s - 1) % NG, (s - 1) // NG)
-                for n in beside.get(s - 1, []):
-                    x_widen(*n)
-                if s == 6:
-                    x_quant(2)
-                if s == 6 + 1:
-                    x_quant(3)
-                    nc.vector.tensor_copy(out=row_sb[:], in_=row_bf[:])
-                h_quant((s - 1) % NG, (s - 1) // NG)
-            g = {2: 0, 4: 1, 5: 2, 7: 3}.get(s)
-            if g is not None:
+        finished = []
+        for s in range(1, len(steps)):
+            first_product(*steps[s])
+            if s in (1, 2):
+                x_quant(2 + 2 * s)
+                x_quant(3 + 2 * s)
+            last_of_quarter = steps[s][1] == NG - 1
+            if steps[s][1] > 0:
+                if last_of_quarter:
+                    h_quant(*steps[s - 1])
+                    times_amp(*steps[s], parts=2)
+                    h_quant(*steps[s], parts=2)
+                else:
+                    times_amp(*steps[s])
+                    h_quant(*steps[s - 1])
+            else:
+                times_amp(*steps[s])
+            fresh = []
+            if s == 2:
                 for u in range(4):
-                    second_product(0, u, [g])
-                if g == NG - 1:
-                    fresh = [(0, u) for u in range(4)]
-            elif s >= 9 and s < NQ * NG:
+                    second_product(0, u, [3])
+                fresh = [(0, u) for u in range(4)]
+            if s >= 6:
                 unit = units.pop(0)
                 second_product(*unit, range(NG))
                 fresh = [unit]
-            for unit in finished[:2]:
+            for unit in finished[:1]:
                 store(*unit, "scalar")
-            finished = finished[2:] + fresh
-            fresh = []
-        last = NQ - 1
+            finished = finished[1:] + fresh
+
         for unit in finished:
             store(*unit, "scalar")
         while len(units) > 1:
             unit = units.pop(0)
             second_product(*unit, range(NG))
-            store(*unit, "scalar" if unit[1] % 2 == 0 else "vector")
-        second_product(last, 3, range(NG))
-        i = NT - 1
-        y = stage.tile([P, 512], F32, tag="y", name="y_t", bufs=2 * NT)
-        y2 = stage.tile([P, 256], F32, tag="y2", name="y2_t", bufs=1)
-        bank = y_bank.pop((last, 3))
-        nc.scalar.activation(out=y[:, 0:256], in_=bank[:, 0:256], func=COPY, scale=row_sb[:, i : i + 1])
-        nc.sync.dma_start(out=out_view[:, i, 512:768], in_=y[:, 0:256])
-        nc.scalar.activation(out=y2[:], in_=bank[:, 256:512], func=COPY, scale=row_sb[:, i : i + 1])
-        nc.sync.dma_start(out=out_view[:, i, 768:1024], in_=y2[:])
+            store(*unit, "scalar")
+        for d0 in (512, 768):
+            bank = psum.tile([P, 256], F32, tag="bank", name="y_last")
+            for g in range(NG):
+                second_pass(bank[:], NQ - 1, 1, g, d0, 256)
+            scale_and_store(bank[:], NT - 1, d0, 256, "scalar")

@@ -89,16 +89,16 @@ def tile_rbf_kernel_readout_d4_kernel(tc, X_bytes, X_scale, C, amp, row, W_words
         for t in (2, 3):
             nc.sync.dma_start(out=c_first[t][:], in_=c_view[0][:, t, :])
         load_c_pair(2)
-        load_x_quarter(1)
         load_c_pair(3)
-        nc.sync.dma_start(out=amp_sb[:], in_=amp.rearrange("(g m t) -> m g t", g=NG, t=4))
         load_c_pair(4)
+        load_x_quarter(1)
+        nc.sync.dma_start(out=amp_sb[:], in_=amp.rearrange("(g m t) -> m g t", g=NG, t=4))
         load_c_pair(5)
-        load_x_quarter(2)
         load_c_pair(6)
+        load_x_quarter(2)
+        load_c_pair(7)
         load_w_scales()
         load_w(0)
-        load_c_pair(7)
         load_x_quarter(3)
         for g in range(1, NG):
             load_w(g)
@@ -276,9 +276,9 @@ def tile_rbf_kernel_readout_d4_kernel(tc, X_bytes, X_scale, C, amp, row, W_words
         c_quant(2)
         c_quant(3)
         first_product(0, 0)
-        x_widen(2)
         c_quant(4)
         c_quant(5)
+        x_widen(2)
 
         for c in range(6, 10):
             c_tile(c)
@@ -286,79 +286,68 @@ def tile_rbf_kernel_readout_d4_kernel(tc, X_bytes, X_scale, C, amp, row, W_words
         c_quant(6)
         c_quant(7)
         first_product(0, 1)
-        times_amp(0, 0)
+        times_amp(0, 0, parts=2)
         c_quant(8)
         c_quant(9)
-        h_quant(0, 0)
 
         for c in range(10, 14):
             c_tile(c)
-        x_widen(4)
+        h_quant(0, 0, parts=2)
         c_quant(10)
         c_quant(11)
-        for u in range(4):
-            second_product(0, u, [0])
         first_product(0, 2)
-        times_amp(0, 1)
+        x_widen(4)
         c_quant(12)
         c_quant(13)
-        h_quant(0, 1)
 
-        c_tile(14)
-        c_tile(15)
         x_tile(2)
         x_tile(3)
-        x_widen(5)
-        c_quant(14)
-        c_quant(15)
-        for u in range(4):
-            second_product(0, u, [1])
-        first_product(0, 3)
-        x_widen(6)
+        c_tile(14)
+        c_tile(15)
+        times_amp(0, 1, parts=2)
         x_quant(2)
         x_quant(3)
+        first_half(0, 3, 0)
+        exponential(0, 3, 0)
+        c_quant(14)
+        c_quant(15)
         first_product(1, 0)
-        times_amp(0, 2)
-        x_widen(7)
-        h_quant(0, 2)
+        first_half(0, 3, 1)
+        exponential(0, 3, 1)
+        h_quant(0, 1, parts=2)
+        times_amp(0, 2, parts=2)
+        x_widen(5)
+        h_quant(0, 2, parts=2)
 
-        for i in range(4, 8):
-            x_tile(i)
-        for u in range(4):
-            second_product(0, u, [2])
-        times_amp(0, 3)
-        nc.vector.tensor_copy(out=row_sb[:], in_=row_bf[:])
-        h_quant(0, 3)
-        times_amp(1, 0)
-
-        steps = [(q, g) for q in range(1, NQ) for g in range(NG)]
+        steps = [(q, g) for q in range(NQ) for g in range(NG)]
         units = [(q, u) for q in range(1, NQ) for u in range(4)]
         finished = []
-        for s in range(1, len(steps)):
-            first_product(*steps[s])
-            if s in (1, 2):
-                x_quant(2 + 2 * s)
-                x_quant(3 + 2 * s)
-            last_of_quarter = steps[s][1] == NG - 1
-            if steps[s][1] > 0:
-                if last_of_quarter:
-                    h_quant(*steps[s - 1])
-                    times_amp(*steps[s], parts=2)
-                    h_quant(*steps[s], parts=2)
-                else:
-                    times_amp(*steps[s])
-                    h_quant(*steps[s - 1])
-            else:
-                times_amp(*steps[s])
+        for s in range(5, len(steps) + 2):
             fresh = []
-            if s == 2:
+            if s == 7:
+                for i in range(4, 8):
+                    x_tile(i)
+            if s in (5, 6, 7, 8):
                 for u in range(4):
-                    second_product(0, u, [3])
-                fresh = [(0, u) for u in range(4)]
-            if s >= 6:
+                    second_product(0, u, [s - 5])
+                if s == 8:
+                    fresh = [(0, u) for u in range(4)]
+            elif s in (11, 12, 14):
                 unit = units.pop(0)
                 second_product(*unit, range(NG))
                 fresh = [unit]
+            if s < len(steps):
+                first_product(*steps[s])
+            if s == 5:
+                x_widen(6)
+                x_widen(7)
+            times_amp(*steps[s - 2], parts=2)
+            if s == 6:
+                nc.vector.tensor_copy(out=row_sb[:], in_=row_bf[:])
+            if s in (7, 8):
+                x_quant(2 * s - 10)
+                x_quant(2 * s - 9)
+            h_quant(*steps[s - 2], parts=2)
             for unit in finished[:1]:
                 store(*unit, "scalar")
             finished = finished[1:] + fresh

@@ -104,7 +104,7 @@ def tile_rbf_kernel_readout_d4_kernel(tc, X_bytes, X_scale, C, amp, row, W_words
             load_w(g)
         nc.sync.dma_start(out=row_bf[:], in_=row.rearrange("(p i) -> p i", i=NT))
 
-        x_bf, x_tr, x_grp, c_tr, c_grp = {}, {}, {}, {}, {}
+        x_bf, x_sorted, x_tr, x_grp, c_tr, c_grp = {}, {}, {}, {}, {}, {}
         z_bank, e_tile, h_grp, y_bank = {}, {}, {}, {}
 
         def spin():
@@ -125,7 +125,7 @@ def tile_rbf_kernel_readout_d4_kernel(tc, X_bytes, X_scale, C, amp, row, W_words
             return tr
 
         def x_widen(i):
-            xb = stage.tile([P, K], BF16, tag="xb", name="xb", bufs=6)
+            xb = stage.tile([P, K], BF16, tag="xb", name="xb", bufs=4)
             x_bf[i] = xb
             for b in range(8):
                 nc.vector.tensor_scalar(
@@ -138,6 +138,19 @@ def tile_rbf_kernel_readout_d4_kernel(tc, X_bytes, X_scale, C, amp, row, W_words
 
         def x_turn(i):
             x_tr[i] = turn(x_bf.pop(i)[:].bitcast(F32))
+
+        def x_sort(i):
+            xs = stage.tile([P, 2, 2, P], F32, tag="xs", name="xs", bufs=4)
+            x_sorted[i] = xs
+            nc.vector.tensor_copy(out=xs[:], in_=x_bf.pop(i)[:].bitcast(F32).rearrange("p (h m u) -> p h u m", h=2, u=2))
+
+        def x_turn_sorted(i):
+            tr = psum.tile([P, 2, 2, P], F32, tag="bank", name="turn_bank")
+            x_tr[i] = tr
+            xs = x_sorted.pop(i)
+            for h in range(2):
+                for u in range(2):
+                    nc.tensor.transpose(tr[:, h, u, :], xs[:, h, u, :], ident[:])
 
         def x_out(i, engine):
             grp = stage.tile([P, 2, P, 4], BF16, tag="grp", name="x_grp_t", align_bytes=64, bufs=8)
@@ -256,6 +269,10 @@ def tile_rbf_kernel_readout_d4_kernel(tc, X_bytes, X_scale, C, amp, row, W_words
             x_turn(i)
             x_out(i, "scalar")
 
+        def x_tile_sorted(i):
+            x_turn_sorted(i)
+            x_out(i, "scalar")
+
         for k in range(3):
             spin()
         x_widen(0)
@@ -286,17 +303,18 @@ def tile_rbf_kernel_readout_d4_kernel(tc, X_bytes, X_scale, C, amp, row, W_words
         c_quant(6)
         c_quant(7)
         first_product(0, 1)
-        times_amp(0, 0, parts=2)
+        times_amp(0, 0)
         c_quant(8)
         c_quant(9)
 
         for c in range(10, 14):
             c_tile(c)
-        h_quant(0, 0, parts=2)
+        h_quant(0, 0)
+        x_widen(4)
         c_quant(10)
         c_quant(11)
         first_product(0, 2)
-        x_widen(4)
+        x_widen(5)
         c_quant(12)
         c_quant(13)
 
@@ -304,7 +322,7 @@ def tile_rbf_kernel_readout_d4_kernel(tc, X_bytes, X_scale, C, amp, row, W_words
         x_tile(3)
         c_tile(14)
         c_tile(15)
-        times_amp(0, 1, parts=2)
+        times_amp(0, 1)
         x_quant(2)
         x_quant(3)
         first_half(0, 3, 0)
@@ -314,10 +332,15 @@ def tile_rbf_kernel_readout_d4_kernel(tc, X_bytes, X_scale, C, amp, row, W_words
         first_product(1, 0)
         first_half(0, 3, 1)
         exponential(0, 3, 1)
-        h_quant(0, 1, parts=2)
-        times_amp(0, 2, parts=2)
-        x_widen(5)
-        h_quant(0, 2, parts=2)
+        h_quant(0, 1)
+        times_amp(0, 2)
+        x_sort(4)
+        x_sort(5)
+        x_widen(6)
+        x_widen(7)
+        x_sort(6)
+        h_quant(0, 2)
+        x_sort(7)
 
         steps = [(q, g) for q in range(NQ) for g in range(NG)]
         units = [(q, u) for q in range(1, NQ) for u in range(4)]
@@ -326,8 +349,8 @@ def tile_rbf_kernel_readout_d4_kernel(tc, X_bytes, X_scale, C, amp, row, W_words
             fresh = []
             if s == 7:
                 for i in range(4, 8):
-                    x_tile(i)
-            if s in (5, 6, 7, 8):
+                    x_tile_sorted(i)
+            if s <= 8:
                 for u in range(4):
                     second_product(0, u, [s - 5])
                 if s == 8:
@@ -338,16 +361,20 @@ def tile_rbf_kernel_readout_d4_kernel(tc, X_bytes, X_scale, C, amp, row, W_words
                 fresh = [unit]
             if s < len(steps):
                 first_product(*steps[s])
-            if s == 5:
-                x_widen(6)
-                x_widen(7)
-            times_amp(*steps[s - 2], parts=2)
-            if s == 6:
-                nc.vector.tensor_copy(out=row_sb[:], in_=row_bf[:])
-            if s in (7, 8):
-                x_quant(2 * s - 10)
-                x_quant(2 * s - 9)
-            h_quant(*steps[s - 2], parts=2)
+            q, g = steps[s - 2]
+            if g == NG - 1 and q > 0:
+                h_quant(q, g - 1)
+                times_amp(q, g, parts=2)
+                h_quant(q, g, parts=2)
+            else:
+                times_amp(q, g)
+                if s == 6:
+                    nc.vector.tensor_copy(out=row_sb[:], in_=row_bf[:])
+                if s in (7, 8):
+                    x_quant(2 * s - 10)
+                    x_quant(2 * s - 9)
+                if s == 6 or g > 0 and q > 0:
+                    h_quant(*steps[s - 3])
             for unit in finished[:1]:
                 store(*unit, "scalar")
             finished = finished[1:] + fresh

@@ -94,8 +94,8 @@ def tile_rbf_kernel_readout_d4_kernel(tc, X_bytes, X_scale, C, amp, row, W_words
         load_x_quarter(1)
         nc.sync.dma_start(out=amp_sb[:], in_=amp.rearrange("(g m t) -> m g t", g=NG, t=4))
         load_c_pair(5)
-        load_c_pair(6)
         load_x_quarter(2)
+        load_c_pair(6)
         load_c_pair(7)
         load_w_scales()
         load_w(0)
@@ -257,17 +257,20 @@ def tile_rbf_kernel_readout_d4_kernel(tc, X_bytes, X_scale, C, amp, row, W_words
             scale_and_store(y_bank.pop((q, u))[:], 2 * q + u // 2, 512 * (u % 2), 512, engine)
 
         def first_product(q, g):
-            for a in range(2):
-                first_half(q, g, a)
-                exponential(q, g, a)
+            half_step(q, g, 0)
+            half_step(q, g, 1)
 
-        def c_tile(c):
+        def half_step(q, g, a):
+            first_half(q, g, a)
+            exponential(q, g, a)
+
+        def c_tile(c, engine="scalar"):
             c_turn(c)
-            c_out(c)
+            c_out(c, engine)
 
-        def x_tile(i):
+        def x_tile(i, engine="scalar"):
             x_turn(i)
-            x_out(i, "scalar")
+            x_out(i, engine)
 
         def x_tile_sorted(i):
             x_turn_sorted(i)
@@ -288,93 +291,100 @@ def tile_rbf_kernel_readout_d4_kernel(tc, X_bytes, X_scale, C, amp, row, W_words
         x_out(1, "vector")
         x_quant(0)
         x_quant(1)
-        for c in range(2, 6):
-            c_tile(c)
-        c_quant(2)
-        c_quant(3)
-        first_product(0, 0)
-        c_quant(4)
-        c_quant(5)
+        c_tile(2)
+        c_tile(3)
+        c_tile(4, "vector")
+        c_tile(5)
+        half_step(0, 0, 0)
+        for c in (2, 3, 4, 5):
+            c_quant(c)
         x_widen(2)
 
-        for c in range(6, 10):
+        for c in range(6, 9):
             c_tile(c)
         x_widen(3)
         c_quant(6)
-        c_quant(7)
-        first_product(0, 1)
-        times_amp(0, 0)
-        c_quant(8)
-        c_quant(9)
-
-        for c in range(10, 14):
-            c_tile(c)
-        h_quant(0, 0)
-        x_widen(4)
-        c_quant(10)
-        c_quant(11)
-        first_product(0, 2)
-        x_widen(5)
-        c_quant(12)
-        c_quant(13)
+        c_tile(9, "vector")
+        half_step(0, 0, 1)
+        half_step(0, 1, 0)
+        for c in range(7, 10):
+            c_quant(c)
 
         x_tile(2)
         x_tile(3)
+        c_tile(10)
+        c_tile(11)
+        x_widen(4)
+        x_widen(5)
+        x_sort(4)
+        half_step(0, 1, 1)
+        half_step(0, 2, 0)
+        x_quant(2)
+        x_sort(5)
+        x_quant(3)
+        c_quant(10)
+        c_quant(11)
+
+        c_tile(12)
+        c_tile(13)
+        x_tile_sorted(4)
+        x_tile_sorted(5)
         c_tile(14)
         c_tile(15)
+        times_amp(0, 0)
+        c_quant(12)
+        h_quant(0, 0)
+        half_step(0, 2, 1)
+        first_product(1, 0)
         times_amp(0, 1)
-        x_quant(2)
-        x_quant(3)
-        first_half(0, 3, 0)
-        exponential(0, 3, 0)
+        c_quant(13)
+        h_quant(0, 1)
+        x_widen(6)
         c_quant(14)
         c_quant(15)
-        first_product(1, 0)
-        first_half(0, 3, 1)
-        exponential(0, 3, 1)
-        h_quant(0, 1)
-        times_amp(0, 2)
-        x_sort(4)
-        x_sort(5)
-        x_widen(6)
         x_widen(7)
+        times_amp(0, 2)
         x_sort(6)
         h_quant(0, 2)
         x_sort(7)
 
-        steps = [(q, g) for q in range(NQ) for g in range(NG)]
+        steps = [(0, 3)] + [(q, g) for q in range(1, NQ) for g in range(NG)]
+        made = steps[:1] + steps[2:]
         units = [(q, u) for q in range(1, NQ) for u in range(4)]
         finished = []
-        for s in range(5, len(steps) + 2):
+        for s in range(len(steps)):
             fresh = []
-            if s == 7:
-                for i in range(4, 8):
-                    x_tile_sorted(i)
-            if s <= 8:
+            if s == 3:
+                x_tile_sorted(6)
+                x_tile_sorted(7)
+            if s < NG:
                 for u in range(4):
-                    second_product(0, u, [s - 5])
-                if s == 8:
+                    second_product(0, u, [s])
+                if s == NG - 1:
                     fresh = [(0, u) for u in range(4)]
-            elif s in (11, 12, 14):
+            elif s in (7, 8, 10):
                 unit = units.pop(0)
                 second_product(*unit, range(NG))
                 fresh = [unit]
-            if s < len(steps):
-                first_product(*steps[s])
-            q, g = steps[s - 2]
+            if s < len(made):
+                first_product(*made[s])
+            q, g = steps[s]
             if g == NG - 1 and q > 0:
                 h_quant(q, g - 1)
                 times_amp(q, g, parts=2)
                 h_quant(q, g, parts=2)
             else:
                 times_amp(q, g)
-                if s == 6:
+                if s == 0:
+                    h_quant(q, g)
+                if s == 1:
                     nc.vector.tensor_copy(out=row_sb[:], in_=row_bf[:])
-                if s in (7, 8):
-                    x_quant(2 * s - 10)
-                    x_quant(2 * s - 9)
-                if s == 6 or g > 0 and q > 0:
-                    h_quant(*steps[s - 3])
+                if s in (1, 2):
+                    x_quant(s + 3)
+                if s in (5, 6):
+                    x_quant(s + 1)
+                if g > 0 and q > 0:
+                    h_quant(*steps[s - 1])
             for unit in finished[:1]:
                 store(*unit, "scalar")
             finished = finished[1:] + fresh

@@ -104,7 +104,7 @@ def tile_rbf_kernel_readout_d4_kernel(tc, X_bytes, X_scale, C, amp, row, W_words
             load_w(g)
         nc.sync.dma_start(out=row_bf[:], in_=row.rearrange("(p i) -> p i", i=NT))
 
-        x_bf, x_sorted, x_tr, x_grp, c_tr, c_grp = {}, {}, {}, {}, {}, {}
+        x_bf, x_tr, x_grp, c_tr, c_grp = {}, {}, {}, {}, {}
         z_bank, e_tile, h_grp, y_bank = {}, {}, {}, {}
 
         def spin():
@@ -125,32 +125,25 @@ def tile_rbf_kernel_readout_d4_kernel(tc, X_bytes, X_scale, C, amp, row, W_words
             return tr
 
         def x_widen(i):
-            xb = stage.tile([P, K], BF16, tag="xb", name="xb", bufs=4)
+            xb = stage.tile([P, 2, 2, P, 2], BF16, tag="xb", name="xb", bufs=4)
             x_bf[i] = xb
             for b in range(8):
+                p0 = 32 * (b % 4)
                 nc.vector.tensor_scalar(
-                    out=xb[:, P * b : P * b + P],
-                    in0=x_bytes(i)[:, P * b : P * b + P].bitcast(F8),
+                    out=xb[:, b // 4, :, p0 : p0 + 32, :].rearrange("p u m e -> p m u e"),
+                    in0=x_bytes(i)[:, P * b : P * b + P].bitcast(F8).rearrange("p (m u e) -> p m u e", u=2, e=2),
                     scalar1=x_sc[:, i, b : b + 1],
                     scalar2=None,
                     op0=MULT,
                 )
 
         def x_turn(i):
-            x_tr[i] = turn(x_bf.pop(i)[:].bitcast(F32))
-
-        def x_sort(i):
-            xs = stage.tile([P, 2, 2, P], F32, tag="xs", name="xs", bufs=4)
-            x_sorted[i] = xs
-            nc.vector.tensor_copy(out=xs[:], in_=x_bf.pop(i)[:].bitcast(F32).rearrange("p (h m u) -> p h u m", h=2, u=2))
-
-        def x_turn_sorted(i):
             tr = psum.tile([P, 2, 2, P], F32, tag="bank", name="turn_bank")
             x_tr[i] = tr
-            xs = x_sorted.pop(i)
+            words = x_bf.pop(i)[:].rearrange("p h u m e -> p h u (m e)").bitcast(F32)
             for h in range(2):
                 for u in range(2):
-                    nc.tensor.transpose(tr[:, h, u, :], xs[:, h, u, :], ident[:])
+                    nc.tensor.transpose(tr[:, h, u, :], words[:, h, u, :], ident[:])
 
         def x_out(i, engine):
             grp = stage.tile([P, 2, P, 4], BF16, tag="grp", name="x_grp_t", align_bytes=64, bufs=8)
@@ -272,9 +265,6 @@ def tile_rbf_kernel_readout_d4_kernel(tc, X_bytes, X_scale, C, amp, row, W_words
             x_turn(i)
             x_out(i, engine)
 
-        def x_tile_sorted(i):
-            x_turn_sorted(i)
-            x_out(i, "scalar")
 
         for k in range(3):
             spin()
@@ -316,19 +306,17 @@ def tile_rbf_kernel_readout_d4_kernel(tc, X_bytes, X_scale, C, amp, row, W_words
         c_tile(11)
         x_widen(4)
         x_widen(5)
-        x_sort(4)
         half_step(0, 1, 1)
         half_step(0, 2, 0)
         x_quant(2)
-        x_sort(5)
         x_quant(3)
         c_quant(10)
         c_quant(11)
 
         c_tile(12)
         c_tile(13)
-        x_tile_sorted(4)
-        x_tile_sorted(5)
+        x_tile(4)
+        x_tile(5)
         c_tile(14)
         c_tile(15)
         times_amp(0, 0)
@@ -344,9 +332,7 @@ def tile_rbf_kernel_readout_d4_kernel(tc, X_bytes, X_scale, C, amp, row, W_words
         c_quant(15)
         x_widen(7)
         times_amp(0, 2)
-        x_sort(6)
         h_quant(0, 2)
-        x_sort(7)
 
         steps = [(0, 3)] + [(q, g) for q in range(1, NQ) for g in range(NG)]
         made = steps[:1] + steps[2:]
@@ -355,8 +341,8 @@ def tile_rbf_kernel_readout_d4_kernel(tc, X_bytes, X_scale, C, amp, row, W_words
         for s in range(len(steps)):
             fresh = []
             if s == 3:
-                x_tile_sorted(6)
-                x_tile_sorted(7)
+                x_tile(6)
+                x_tile(7)
             if s < NG:
                 for u in range(4):
                     second_product(0, u, [s])

@@ -37,8 +37,8 @@ def tile_rbf_kernel_readout_d4_kernel(tc, X_bytes, X_scale, C, amp, row, W_words
         x_raw = [keep.tile([P, K], U8, name="x_raw%d" % i) for i in range(2)]
         x_raw_late = [keep.tile([P, 2, K], U8, name="x_raw_late%d" % q) for q in range(1, NQ)]
         x_sc = keep.tile([P, NT, 8], F32, name="x_sc")
-        c_first = [keep.tile([P, K], BF16, name="c_first%d" % t) for t in range(4)]
-        c_pairs = [keep.tile([P, 2, K], BF16, name="c_pairs%d" % n) for n in range(2, 2 * NG)]
+        c_first = [keep.tile([P, K], BF16, name="c_first%d" % t) for t in range(6)]
+        c_pairs = [keep.tile([P, 2, K], BF16, name="c_pairs%d" % n) for n in range(3, 2 * NG)]
         amp_sb = keep.tile([P, NG, 4], BF16, name="amp_sb")
         row_bf = keep.tile([P, NT], BF16, name="row_bf")
         row_sb = keep.tile([P, NT], F32, name="row_sb")
@@ -63,10 +63,13 @@ def tile_rbf_kernel_readout_d4_kernel(tc, X_bytes, X_scale, C, amp, row, W_words
             return x_raw[i][:] if i < 2 else x_raw_late[i // 2 - 1][:, i % 2, :]
 
         def c_rows(c):
-            return c_first[c][:] if c < 4 else c_pairs[c // 2 - 2][:, c % 2, :]
+            return c_first[c][:] if c < 6 else c_pairs[c // 2 - 3][:, c % 2, :]
+
+        def load_c_tile(c):
+            nc.sync.dma_start(out=c_first[c][:], in_=c_view[c // 4][:, c % 4, :])
 
         def load_c_pair(n):
-            nc.sync.dma_start(out=c_pairs[n - 2][:], in_=c_view[n // 2][:, 2 * (n % 2) : 2 * (n % 2) + 2, :])
+            nc.sync.dma_start(out=c_pairs[n - 3][:], in_=c_view[n // 2][:, 2 * (n % 2) : 2 * (n % 2) + 2, :])
 
         def load_x_quarter(q):
             nc.sync.dma_start(out=x_raw_late[q - 1][:], in_=x_view[:, 2 * q : 2 * q + 2, :])
@@ -81,26 +84,24 @@ def tile_rbf_kernel_readout_d4_kernel(tc, X_bytes, X_scale, C, amp, row, W_words
                     in_=W_scales[:, 4 * r : 4 * r + 4, :].rearrange("g r n -> r g n").bitcast(I32),
                 )
 
-        nc.sync.dma_start(out=c_first[0][:], in_=c_view[0][:, 0, :])
+        load_c_tile(0)
         nc.sync.dma_start(out=x_sc[:], in_=X_scale.rearrange("(p i) b -> p i b", i=NT))
         nc.sync.dma_start(out=x_raw[0][:], in_=x_view[:, 0, :])
-        nc.sync.dma_start(out=c_first[1][:], in_=c_view[0][:, 1, :])
+        load_c_tile(1)
         nc.sync.dma_start(out=x_raw[1][:], in_=x_view[:, 1, :])
-        for t in (2, 3):
-            nc.sync.dma_start(out=c_first[t][:], in_=c_view[0][:, t, :])
-        load_c_pair(2)
-        load_c_pair(3)
-        load_c_pair(4)
+        for c in range(2, 6):
+            load_c_tile(c)
+        for n in range(3, 5):
+            load_c_pair(n)
         load_x_quarter(1)
-        nc.sync.dma_start(out=amp_sb[:], in_=amp.rearrange("(g m t) -> m g t", g=NG, t=4))
         load_c_pair(5)
         load_x_quarter(2)
         load_c_pair(6)
         load_c_pair(7)
-        load_w_scales()
-        load_w(0)
         load_x_quarter(3)
-        for g in range(1, NG):
+        nc.sync.dma_start(out=amp_sb[:], in_=amp.rearrange("(g m t) -> m g t", g=NG, t=4))
+        load_w_scales()
+        for g in range(NG):
             load_w(g)
         nc.sync.dma_start(out=row_bf[:], in_=row.rearrange("(p i) -> p i", i=NT))
 
@@ -275,13 +276,14 @@ def tile_rbf_kernel_readout_d4_kernel(tc, X_bytes, X_scale, C, amp, row, W_words
         c_tile(1)
         x_tile(0)
         c_quant(0)
-        x_turn(1)
         spin()
+        x_turn(1)
         c_quant(1)
         x_out(1, "vector")
         x_quant(0)
         x_quant(1)
         c_tile(2)
+        spin()
         c_tile(3)
         c_tile(4, "vector")
         c_tile(5)
@@ -300,77 +302,67 @@ def tile_rbf_kernel_readout_d4_kernel(tc, X_bytes, X_scale, C, amp, row, W_words
         for c in range(7, 10):
             c_quant(c)
 
-        x_tile(2)
-        x_tile(3)
         c_tile(10)
-        c_tile(11)
+        x_tile(2)
         x_widen(4)
-        x_widen(5)
-        half_step(0, 1, 1)
-        half_step(0, 2, 0)
+        x_tile(3, "vector")
+        for c in range(11, 14):
+            c_tile(c)
+        c_quant(10)
         x_quant(2)
         x_quant(3)
-        c_quant(10)
         c_quant(11)
+        half_step(0, 1, 1)
+        first_product(0, 2)
+        first_product(1, 0)
+        for i in range(5, 8):
+            x_widen(i)
+        c_quant(12)
+        c_quant(13)
 
-        c_tile(12)
-        c_tile(13)
-        x_tile(4)
-        x_tile(5)
         c_tile(14)
         c_tile(15)
         times_amp(0, 0)
-        c_quant(12)
+        x_tile(4, "vector")
+        for i in range(5, 8):
+            x_tile(i)
         h_quant(0, 0)
-        half_step(0, 2, 1)
-        first_product(1, 0)
-        times_amp(0, 1)
-        c_quant(13)
-        h_quant(0, 1)
-        x_widen(6)
         c_quant(14)
         c_quant(15)
-        x_widen(7)
-        times_amp(0, 2)
-        h_quant(0, 2)
 
-        steps = [(0, 3)] + [(q, g) for q in range(1, NQ) for g in range(NG)]
-        made = steps[:1] + steps[2:]
+        steps = [(q, g) for q in range(NQ) for g in range(NG)]
+        made = [(1, 1), (0, 3)] + steps[6:]
         units = [(q, u) for q in range(1, NQ) for u in range(4)]
         finished = []
-        for s in range(len(steps)):
+        for s in range(1, len(steps)):
             fresh = []
-            if s == 3:
-                x_tile(6)
-                x_tile(7)
-            if s < NG:
+            if s <= len(made):
+                first_product(*made[s - 1])
+            if s <= NG:
                 for u in range(4):
-                    second_product(0, u, [s])
-                if s == NG - 1:
+                    second_product(0, u, [s - 1])
+                if s == NG:
                     fresh = [(0, u) for u in range(4)]
-            elif s in (7, 8, 10):
+            elif s >= 8 and s <= len(made):
                 unit = units.pop(0)
                 second_product(*unit, range(NG))
                 fresh = [unit]
-            if s < len(made):
-                first_product(*made[s])
             q, g = steps[s]
             if g == NG - 1 and q > 0:
                 h_quant(q, g - 1)
                 times_amp(q, g, parts=2)
                 h_quant(q, g, parts=2)
+            elif q == 0:
+                times_amp(q, g)
+                x_quant(3 + s)
+                h_quant(q, g)
             else:
                 times_amp(q, g)
-                if s == 0:
-                    h_quant(q, g)
-                if s == 1:
+                if s == 4:
+                    x_quant(7)
                     nc.vector.tensor_copy(out=row_sb[:], in_=row_bf[:])
-                if s in (1, 2):
-                    x_quant(s + 3)
-                if s in (5, 6):
-                    x_quant(s + 1)
-                if g > 0 and q > 0:
-                    h_quant(*steps[s - 1])
+                if g > 0:
+                    h_quant(q, g - 1)
             for unit in finished[:1]:
                 store(*unit, "scalar")
             finished = finished[1:] + fresh

@@ -112,12 +112,6 @@ def tile_rbf_kernel_readout_d4_kernel(tc, X_bytes, X_scale, C, amp, row, W_words
             bank = psum.tile([P, 512], F32, tag="bank", name="warm_bank")
             nc.tensor.matmul(bank[:], lhsT=warm[:, 0:P], rhs=warm[:], start=True, stop=True)
 
-        def copy_out(engine, dst, src):
-            if engine == "vector":
-                nc.vector.tensor_copy(out=dst, in_=src)
-            else:
-                nc.scalar.copy(out=dst, in_=src)
-
         def turn(words):
             tr = psum.tile([P, 2, 2, P], F32, tag="bank", name="turn_bank")
             for h in range(2):
@@ -146,10 +140,10 @@ def tile_rbf_kernel_readout_d4_kernel(tc, X_bytes, X_scale, C, amp, row, W_words
                 for u in range(2):
                     nc.tensor.transpose(tr[:, h, u, :], words[:, h, u, :], ident[:])
 
-        def x_out(i, engine):
+        def x_out(i):
             grp = stage.tile([P, 2, P, 4], BF16, tag="grp", name="x_grp_t", align_bytes=64, bufs=8)
             x_grp[i] = grp
-            copy_out(engine, grp[:].bitcast(F32), x_tr.pop(i)[:].rearrange("p h u m -> p h m u"))
+            nc.scalar.copy(out=grp[:].bitcast(F32), in_=x_tr.pop(i)[:].rearrange("p h u m -> p h m u"))
 
         def x_quant(i):
             grp = x_grp.pop(i)
@@ -164,10 +158,10 @@ def tile_rbf_kernel_readout_d4_kernel(tc, X_bytes, X_scale, C, amp, row, W_words
         def c_turn(c):
             c_tr[c] = turn(c_rows(c).bitcast(F32))
 
-        def c_out(c, engine="scalar"):
+        def c_out(c):
             grp = stage.tile([P, 2, P, 4], BF16, tag="grp", name="c_grp_t", align_bytes=64, bufs=8)
             c_grp[c] = grp
-            copy_out(engine, grp[:].bitcast(F32), c_tr.pop(c)[:].rearrange("p h u m -> p h m u"))
+            nc.scalar.copy(out=grp[:].bitcast(F32), in_=c_tr.pop(c)[:].rearrange("p h u m -> p h m u"))
 
         def c_quant(c):
             nc.vector.quantize_mx(
@@ -258,13 +252,13 @@ def tile_rbf_kernel_readout_d4_kernel(tc, X_bytes, X_scale, C, amp, row, W_words
             first_half(q, g, a)
             exponential(q, g, a)
 
-        def c_tile(c, engine="scalar"):
+        def c_tile(c):
             c_turn(c)
-            c_out(c, engine)
+            c_out(c)
 
-        def x_tile(i, engine="scalar"):
+        def x_tile(i):
             x_turn(i)
-            x_out(i, engine)
+            x_out(i)
 
 
         for k in range(3):
@@ -279,13 +273,13 @@ def tile_rbf_kernel_readout_d4_kernel(tc, X_bytes, X_scale, C, amp, row, W_words
         spin()
         x_turn(1)
         c_quant(1)
-        x_out(1, "vector")
+        x_out(1)
         x_quant(0)
         x_quant(1)
         c_tile(2)
         spin()
         c_tile(3)
-        c_tile(4, "vector")
+        c_tile(4)
         c_tile(5)
         half_step(0, 0, 0)
         for c in (2, 3, 4, 5):
@@ -296,7 +290,7 @@ def tile_rbf_kernel_readout_d4_kernel(tc, X_bytes, X_scale, C, amp, row, W_words
             c_tile(c)
         x_widen(3)
         c_quant(6)
-        c_tile(9, "vector")
+        c_tile(9)
         half_step(0, 0, 1)
         half_step(0, 1, 0)
         for c in range(7, 10):
@@ -305,7 +299,7 @@ def tile_rbf_kernel_readout_d4_kernel(tc, X_bytes, X_scale, C, amp, row, W_words
         c_tile(10)
         x_tile(2)
         x_widen(4)
-        x_tile(3, "vector")
+        x_tile(3)
         for c in range(11, 14):
             c_tile(c)
         c_quant(10)
@@ -313,8 +307,9 @@ def tile_rbf_kernel_readout_d4_kernel(tc, X_bytes, X_scale, C, amp, row, W_words
         x_quant(3)
         c_quant(11)
         half_step(0, 1, 1)
-        first_product(0, 2)
+        half_step(0, 2, 0)
         first_product(1, 0)
+        half_step(0, 2, 1)
         for i in range(5, 8):
             x_widen(i)
         c_quant(12)
@@ -323,7 +318,7 @@ def tile_rbf_kernel_readout_d4_kernel(tc, X_bytes, X_scale, C, amp, row, W_words
         c_tile(14)
         c_tile(15)
         times_amp(0, 0)
-        x_tile(4, "vector")
+        x_tile(4)
         for i in range(5, 8):
             x_tile(i)
         h_quant(0, 0)

@@ -95,11 +95,11 @@ def tile_rbf_kernel_readout_d4_kernel(tc, X_bytes, X_scale, C, amp, row, W_words
             load_c_pair(n)
         load_x_quarter(1)
         load_c_pair(5)
-        load_x_quarter(2)
+        nc.sync.dma_start(out=amp_sb[:], in_=amp.rearrange("(g m t) -> m g t", g=NG, t=4))
         load_c_pair(6)
+        load_x_quarter(2)
         load_c_pair(7)
         load_x_quarter(3)
-        nc.sync.dma_start(out=amp_sb[:], in_=amp.rearrange("(g m t) -> m g t", g=NG, t=4))
         load_w_scales()
         for g in range(NG):
             load_w(g)
@@ -108,37 +108,40 @@ def tile_rbf_kernel_readout_d4_kernel(tc, X_bytes, X_scale, C, amp, row, W_words
         x_bf, x_tr, x_grp, c_tr, c_grp = {}, {}, {}, {}, {}
         z_bank, e_tile, h_grp, y_bank = {}, {}, {}, {}
 
-        def spin():
-            bank = psum.tile([P, 512], F32, tag="bank", name="warm_bank")
-            nc.tensor.matmul(bank[:], lhsT=warm[:, 0:P], rhs=warm[:], start=True, stop=True)
+        def spin(bank):
+            nc.tensor.matmul(bank, lhsT=warm[:, 0:P], rhs=warm[:], start=True, stop=True)
 
-        def turn(words):
+        def turn(word_sets, dummies=0):
             tr = psum.tile([P, 2, 2, P], F32, tag="bank", name="turn_bank")
+            for k in range(dummies):
+                spin(tr[:].rearrange("p h u m -> p (h u m)"))
             for h in range(2):
                 for u in range(2):
-                    nc.tensor.transpose(tr[:, h, u, :], words[:, 256 * h + u : 256 * (h + 1) : 2], ident[:])
+                    nc.tensor.transpose(tr[:, h, u, :], word_sets(h, u), ident[:])
             return tr
 
+        def every_second_word(words):
+            return lambda h, u: words[:, 256 * h + u : 256 * (h + 1) : 2]
+
         def x_widen(i):
-            xb = stage.tile([P, 2, 2, P, 2], BF16, tag="xb", name="xb", bufs=4)
+            xb = stage.tile([P, K], BF16, tag="xb", name="xb", bufs=4)
             x_bf[i] = xb
             for b in range(8):
-                p0 = 32 * (b % 4)
-                nc.vector.tensor_scalar(
-                    out=xb[:, b // 4, :, p0 : p0 + 32, :].rearrange("p u m e -> p m u e"),
-                    in0=x_bytes(i)[:, P * b : P * b + P].bitcast(F8).rearrange("p (m u e) -> p m u e", u=2, e=2),
-                    scalar1=x_sc[:, i, b : b + 1],
-                    scalar2=None,
-                    op0=MULT,
-                )
+                src = x_bytes(i)[:, P * b : P * b + P].bitcast(F8)
+                if i < 2:
+                    dst = xb[:, P * b : P * b + P]
+                else:
+                    p0 = 32 * (b % 4)
+                    dst = xb[:].rearrange("p (h u m e) -> p h m u e", h=2, u=2, e=2)[:, b // 4, p0 : p0 + 32]
+                    src = src.rearrange("p (m u e) -> p m u e", u=2, e=2)
+                nc.vector.tensor_scalar(out=dst, in0=src, scalar1=x_sc[:, i, b : b + 1], scalar2=None, op0=MULT)
 
-        def x_turn(i):
-            tr = psum.tile([P, 2, 2, P], F32, tag="bank", name="turn_bank")
-            x_tr[i] = tr
-            words = x_bf.pop(i)[:].rearrange("p h u m e -> p h u (m e)").bitcast(F32)
-            for h in range(2):
-                for u in range(2):
-                    nc.tensor.transpose(tr[:, h, u, :], words[:, h, u, :], ident[:])
+        def x_turn(i, dummies):
+            words = x_bf.pop(i)[:].bitcast(F32)
+            if i < 2:
+                x_tr[i] = turn(every_second_word(words), dummies)
+            else:
+                x_tr[i] = turn(lambda h, u: words[:, 256 * h + P * u : 256 * h + P * (u + 1)], dummies)
 
         def x_out(i):
             grp = stage.tile([P, 2, P, 4], BF16, tag="grp", name="x_grp_t", align_bytes=64, bufs=8)
@@ -155,8 +158,8 @@ def tile_rbf_kernel_readout_d4_kernel(tc, X_bytes, X_scale, C, amp, row, W_words
                     in_=grp[:, h, :, :].rearrange("p m j -> p (m j)"),
                 )
 
-        def c_turn(c):
-            c_tr[c] = turn(c_rows(c).bitcast(F32))
+        def c_turn(c, dummies):
+            c_tr[c] = turn(every_second_word(c_rows(c).bitcast(F32)), dummies)
 
         def c_out(c):
             grp = stage.tile([P, 2, P, 4], BF16, tag="grp", name="c_grp_t", align_bytes=64, bufs=8)
@@ -252,110 +255,109 @@ def tile_rbf_kernel_readout_d4_kernel(tc, X_bytes, X_scale, C, amp, row, W_words
             first_half(q, g, a)
             exponential(q, g, a)
 
-        def c_tile(c):
-            c_turn(c)
+        def c_tile(c, dummies=0):
+            c_turn(c, dummies)
             c_out(c)
 
-        def x_tile(i):
-            x_turn(i)
+        def x_tile(i, dummies=0):
+            x_turn(i, dummies)
             x_out(i)
 
+        def scale_and_quantise(q, g):
+            times_amp(q, g)
+            h_quant(q, g)
 
-        for k in range(3):
-            spin()
         x_widen(0)
         x_widen(1)
-        c_tile(0)
-        spin()
-        c_tile(1)
+        c_tile(0, dummies=3)
+        c_tile(1, dummies=1)
         x_tile(0)
-        c_quant(0)
-        spin()
-        x_turn(1)
-        c_quant(1)
-        x_out(1)
-        x_quant(0)
-        x_quant(1)
-        c_tile(2)
-        spin()
-        c_tile(3)
-        c_tile(4)
-        c_tile(5)
-        half_step(0, 0, 0)
-        for c in (2, 3, 4, 5):
-            c_quant(c)
-        x_widen(2)
-
-        for c in range(6, 9):
+        x_tile(1)
+        for i in range(2):
+            c_quant(i)
+        for i in range(2):
+            x_quant(i)
+        c_tile(2, dummies=1)
+        for c in range(3, 6):
             c_tile(c)
+        half_step(0, 0, 0)
+        for c in range(2, 6):
+            c_quant(c)
+
+        for c in range(6, 10):
+            c_tile(c)
+        x_widen(2)
         x_widen(3)
-        c_quant(6)
-        c_tile(9)
         half_step(0, 0, 1)
         half_step(0, 1, 0)
-        for c in range(7, 10):
+        for c in range(6, 10):
             c_quant(c)
+        scale_and_quantise(0, 0)
 
         c_tile(10)
+        c_tile(11)
         x_tile(2)
+        x_tile(3, dummies=1)
+        c_tile(12)
+        c_tile(13)
         x_widen(4)
-        x_tile(3)
-        for c in range(11, 14):
-            c_tile(c)
-        c_quant(10)
-        x_quant(2)
-        x_quant(3)
-        c_quant(11)
         half_step(0, 1, 1)
         half_step(0, 2, 0)
-        first_product(1, 0)
-        half_step(0, 2, 1)
-        for i in range(5, 8):
-            x_widen(i)
+        c_quant(10)
+        c_quant(11)
+        x_quant(2)
+        x_quant(3)
         c_quant(12)
         c_quant(13)
 
         c_tile(14)
         c_tile(15)
-        times_amp(0, 0)
         x_tile(4)
-        for i in range(5, 8):
-            x_tile(i)
-        h_quant(0, 0)
+        for i in range(5, NT):
+            x_widen(i)
+        half_step(0, 2, 1)
+        half_step(0, 3, 0)
+        first_product(1, 0)
+        first_product(1, 1)
         c_quant(14)
         c_quant(15)
+        x_quant(4)
+        scale_and_quantise(0, 1)
+        scale_and_quantise(0, 2)
+
+        for i in range(5, NT):
+            x_tile(i)
+        half_step(0, 3, 1)
+        for i in range(5, NT):
+            x_quant(i)
+        nc.vector.tensor_copy(out=row_sb[:], in_=row_bf[:])
 
         steps = [(q, g) for q in range(NQ) for g in range(NG)]
-        made = [(1, 1), (0, 3)] + steps[6:]
+        to_make, to_scale = steps[NG + 2 :], steps[NG - 1 :]
         units = [(q, u) for q in range(1, NQ) for u in range(4)]
-        finished = []
-        for s in range(1, len(steps)):
+        quantised, finished = 0, []
+        for u in range(4):
+            second_product(0, u, [0])
+        for k, (q, g) in enumerate(to_scale):
             fresh = []
-            if s <= len(made):
-                first_product(*made[s - 1])
-            if s <= NG:
-                for u in range(4):
-                    second_product(0, u, [s - 1])
-                if s == NG:
-                    fresh = [(0, u) for u in range(4)]
-            elif s >= 8 and s <= len(made):
-                unit = units.pop(0)
-                second_product(*unit, range(NG))
-                fresh = [unit]
-            q, g = steps[s]
-            if g == NG - 1 and q > 0:
-                h_quant(q, g - 1)
+            if k < len(to_make):
+                first_product(*to_make[k])
+                if k + 1 < NG:
+                    for u in range(4):
+                        second_product(0, u, [k + 1])
+                    if k + 2 == NG:
+                        fresh = [(0, u) for u in range(4)]
+                elif units[0][0] <= quantised:
+                    fresh = [units.pop(0)]
+                    second_product(*fresh[0], range(NG))
+            if g == NG - 1:
+                if q > 0:
+                    h_quant(q, g - 1)
                 times_amp(q, g, parts=2)
                 h_quant(q, g, parts=2)
-            elif q == 0:
-                times_amp(q, g)
-                x_quant(3 + s)
-                h_quant(q, g)
+                quantised = q
             else:
                 times_amp(q, g)
-                if s == 4:
-                    x_quant(7)
-                    nc.vector.tensor_copy(out=row_sb[:], in_=row_bf[:])
                 if g > 0:
                     h_quant(q, g - 1)
             for unit in finished[:1]:

@@ -108,13 +108,11 @@ def tile_rbf_kernel_readout_d4_kernel(tc, X_bytes, X_scale, C, amp, row, W_words
         x_bf, x_tr, x_grp, c_tr, c_grp = {}, {}, {}, {}, {}
         z_bank, e_tile, h_grp, y_bank = {}, {}, {}, {}
 
-        def spin(bank):
-            nc.tensor.matmul(bank, lhsT=warm[:, 0:P], rhs=warm[:], start=True, stop=True)
-
-        def turn(word_sets, dummies=0):
-            tr = psum.tile([P, 2, 2, P], F32, tag="bank", name="turn_bank")
+        def turn(word_sets, dummies):
             for k in range(dummies):
-                spin(tr[:].rearrange("p h u m -> p (h u m)"))
+                bank = psum.tile([P, 512], F32, tag="bank", name="warm_bank")
+                nc.tensor.matmul(bank[:], lhsT=warm[:, 0:P], rhs=warm[:], start=True, stop=True)
+            tr = psum.tile([P, 2, 2, P], F32, tag="bank", name="turn_bank")
             for h in range(2):
                 for u in range(2):
                     nc.tensor.transpose(tr[:, h, u, :], word_sets(h, u), ident[:])
@@ -122,6 +120,12 @@ def tile_rbf_kernel_readout_d4_kernel(tc, X_bytes, X_scale, C, amp, row, W_words
 
         def every_second_word(words):
             return lambda h, u: words[:, 256 * h + u : 256 * (h + 1) : 2]
+
+        def copy_out(on_vector, dst, src):
+            if on_vector:
+                nc.vector.tensor_copy(out=dst, in_=src)
+            else:
+                nc.scalar.copy(out=dst, in_=src)
 
         def x_widen(i):
             xb = stage.tile([P, K], BF16, tag="xb", name="xb", bufs=4)
@@ -143,10 +147,10 @@ def tile_rbf_kernel_readout_d4_kernel(tc, X_bytes, X_scale, C, amp, row, W_words
             else:
                 x_tr[i] = turn(lambda h, u: words[:, 256 * h + P * u : 256 * h + P * (u + 1)], dummies)
 
-        def x_out(i):
+        def x_out(i, on_vector):
             grp = stage.tile([P, 2, P, 4], BF16, tag="grp", name="x_grp_t", align_bytes=64, bufs=8)
             x_grp[i] = grp
-            nc.scalar.copy(out=grp[:].bitcast(F32), in_=x_tr.pop(i)[:].rearrange("p h u m -> p h m u"))
+            copy_out(on_vector, grp[:].bitcast(F32), x_tr.pop(i)[:].rearrange("p h u m -> p h m u"))
 
         def x_quant(i):
             grp = x_grp.pop(i)
@@ -161,10 +165,10 @@ def tile_rbf_kernel_readout_d4_kernel(tc, X_bytes, X_scale, C, amp, row, W_words
         def c_turn(c, dummies):
             c_tr[c] = turn(every_second_word(c_rows(c).bitcast(F32)), dummies)
 
-        def c_out(c):
+        def c_out(c, on_vector):
             grp = stage.tile([P, 2, P, 4], BF16, tag="grp", name="c_grp_t", align_bytes=64, bufs=8)
             c_grp[c] = grp
-            nc.scalar.copy(out=grp[:].bitcast(F32), in_=c_tr.pop(c)[:].rearrange("p h u m -> p h m u"))
+            copy_out(on_vector, grp[:].bitcast(F32), c_tr.pop(c)[:].rearrange("p h u m -> p h m u"))
 
         def c_quant(c):
             nc.vector.quantize_mx(
@@ -255,26 +259,30 @@ def tile_rbf_kernel_readout_d4_kernel(tc, X_bytes, X_scale, C, amp, row, W_words
             first_half(q, g, a)
             exponential(q, g, a)
 
-        def c_tile(c, dummies=0):
+        def c_tile(c, dummies=0, on_vector=False):
             c_turn(c, dummies)
-            c_out(c)
+            c_out(c, on_vector)
 
-        def x_tile(i, dummies=0):
+        def x_tile(i, dummies=0, on_vector=False):
             x_turn(i, dummies)
-            x_out(i)
+            x_out(i, on_vector)
 
         def scale_and_quantise(q, g):
             times_amp(q, g)
             h_quant(q, g)
+
+        def second_group(g):
+            for u in range(4):
+                second_product(0, u, [g])
 
         x_widen(0)
         x_widen(1)
         c_tile(0, dummies=3)
         c_tile(1, dummies=1)
         x_tile(0)
-        x_tile(1)
         for i in range(2):
             c_quant(i)
+        x_tile(1, on_vector=True)
         for i in range(2):
             x_quant(i)
         c_tile(2, dummies=1)
@@ -284,10 +292,10 @@ def tile_rbf_kernel_readout_d4_kernel(tc, X_bytes, X_scale, C, amp, row, W_words
         for c in range(2, 6):
             c_quant(c)
 
-        for c in range(6, 10):
-            c_tile(c)
         x_widen(2)
         x_widen(3)
+        for c in range(6, 10):
+            c_tile(c, on_vector=(c == 9))
         half_step(0, 0, 1)
         half_step(0, 1, 0)
         for c in range(6, 10):
@@ -318,41 +326,40 @@ def tile_rbf_kernel_readout_d4_kernel(tc, X_bytes, X_scale, C, amp, row, W_words
         half_step(0, 2, 1)
         half_step(0, 3, 0)
         first_product(1, 0)
-        first_product(1, 1)
+        second_group(0)
+        scale_and_quantise(0, 1)
         c_quant(14)
         c_quant(15)
         x_quant(4)
-        scale_and_quantise(0, 1)
+        first_product(1, 1)
+        half_step(0, 3, 1)
+        second_group(1)
         scale_and_quantise(0, 2)
 
         for i in range(5, NT):
             x_tile(i)
-        half_step(0, 3, 1)
+        second_group(2)
+        scale_and_quantise(0, 3)
         for i in range(5, NT):
             x_quant(i)
         nc.vector.tensor_copy(out=row_sb[:], in_=row_bf[:])
 
-        steps = [(q, g) for q in range(NQ) for g in range(NG)]
-        to_make, to_scale = steps[NG + 2 :], steps[NG - 1 :]
+        steps = [(q, g) for q in range(1, NQ) for g in range(NG)]
+        to_make, to_scale = steps[2:], steps
         units = [(q, u) for q in range(1, NQ) for u in range(4)]
         quantised, finished = 0, []
-        for u in range(4):
-            second_product(0, u, [0])
         for k, (q, g) in enumerate(to_scale):
             fresh = []
             if k < len(to_make):
                 first_product(*to_make[k])
-                if k + 1 < NG:
-                    for u in range(4):
-                        second_product(0, u, [k + 1])
-                    if k + 2 == NG:
-                        fresh = [(0, u) for u in range(4)]
+                if k == 0:
+                    second_group(NG - 1)
+                    fresh = [(0, u) for u in range(4)]
                 elif units[0][0] <= quantised:
                     fresh = [units.pop(0)]
                     second_product(*fresh[0], range(NG))
             if g == NG - 1:
-                if q > 0:
-                    h_quant(q, g - 1)
+                h_quant(q, g - 1)
                 times_amp(q, g, parts=2)
                 h_quant(q, g, parts=2)
                 quantised = q

from contextlib import ExitStack

import concourse.mybir as mybir
from concourse.masks import make_identity

T, K, J, D = 1024, 1024, 2048, 1024
FLOPS = 2 * T * K * J + 2 * T * J * D

F32 = mybir.dt.float32
BF16 = mybir.dt.bfloat16
U32 = mybir.dt.uint32
I32 = mybir.dt.int32
U8 = mybir.dt.uint8
F8 = mybir.dt.float8_e4m3fn
FP8X4 = mybir.dt.float8_e4m3fn_x4
FP4X4 = mybir.dt.float4_e2m1fn_x4
MULT = mybir.AluOpType.mult
EXP = mybir.ActivationFunctionType.Exp
COPY = mybir.ActivationFunctionType.Copy

P = 128
NT = T // P
NQ = 4
QT = T // NQ
NG = J // 512


def tile_rbf_kernel_readout_d4_kernel(tc, X_bytes, X_scale, C, amp, row, W_words, W_scales, out):
    nc = tc.nc
    with ExitStack() as ctx:
        keep = ctx.enter_context(tc.tile_pool(name="keep", bufs=1))
        stage = ctx.enter_context(tc.tile_pool(name="stage", bufs=3))
        psum = ctx.enter_context(tc.psum_pool(name="psum", bufs=8))
        ctx.enter_context(tc.manual_schedule())

        ident = keep.tile([P, P], F32, name="ident")
        x_raw = [keep.tile([P, K], U8, name="x_raw%d" % i) for i in range(2)]
        x_raw_late = [keep.tile([P, 2, K], U8, name="x_raw_late%d" % q) for q in range(1, NQ)]
        x_sc = keep.tile([P, NT, 8], F32, name="x_sc")
        c_first = [keep.tile([P, K], BF16, name="c_first%d" % t) for t in range(6)]
        c_pairs = [keep.tile([P, 2, K], BF16, name="c_pairs%d" % n) for n in range(3, 2 * NG)]
        amp_sb = keep.tile([P, NG, 4], BF16, name="amp_sb")
        row_bf = keep.tile([P, NT], BF16, name="row_bf")
        row_sb = keep.tile([P, NT], F32, name="row_sb")
        w_sb = [keep.tile([P, 2 * D], U8, name="w_sb%d" % g, align_bytes=64) for g in range(NG)]
        w_sc = keep.tile([P, NG, D], U8, name="w_sc", align_bytes=64)
        x_codes = [keep.tile([P, 2, QT], U32, name="x_codes%d" % q, align_bytes=64) for q in range(NQ)]
        x_planes = [keep.tile([P, 2, QT], U8, name="x_planes%d" % q, align_bytes=64) for q in range(NQ)]
        c_codes = [keep.tile([P, 2, P], U32, name="c_codes%d" % c, align_bytes=64) for c in range(4 * NG)]
        c_planes = [keep.tile([P, 2, P], U8, name="c_planes%d" % c, align_bytes=64) for c in range(4 * NG)]
        h_codes = [[keep.tile([P, QT], U32, name="h_codes%d_%d" % (q, g), align_bytes=64) for g in range(NG)] for q in range(NQ)]
        h_planes = [[keep.tile([P, QT], U8, name="h_planes%d_%d" % (q, g), align_bytes=64) for g in range(NG)] for q in range(NQ)]

        make_identity(nc, ident[:])
        warm = keep.tile([P, 512], BF16, name="warm")
        nc.vector.memset(warm[:], 0.0)
        nc.vector.memset(w_sc[:].rearrange("p g n -> p (g n)").bitcast(I32), 0)

        x_view = X_bytes.rearrange("(p i) k -> p i k", i=NT)
        c_view = C.rearrange("(g m t) k -> g m t k", g=NG, t=4)

        def x_bytes(i):
            return x_raw[i][:] if i < 2 else x_raw_late[i // 2 - 1][:, i % 2, :]

        def c_rows(c):
            return c_first[c][:] if c < 6 else c_pairs[c // 2 - 3][:, c % 2, :]

        def load_c_tile(c):
            nc.sync.dma_start(out=c_first[c][:], in_=c_view[c // 4][:, c % 4, :])

        def load_c_pair(n):
            nc.sync.dma_start(out=c_pairs[n - 3][:], in_=c_view[n // 2][:, 2 * (n % 2) : 2 * (n % 2) + 2, :])

        def load_x_quarter(q):
            nc.sync.dma_start(out=x_raw_late[q - 1][:], in_=x_view[:, 2 * q : 2 * q + 2, :])

        def load_w(g):
            nc.sync.dma_start(out=w_sb[g][:].bitcast(I32), in_=W_words[g].bitcast(I32))

        def load_w_scales():
            for r in range(4):
                nc.sync.dma_start(
                    out=w_sc[32 * r : 32 * r + 4, :, :].bitcast(I32),
                    in_=W_scales[:, 4 * r : 4 * r + 4, :].rearrange("g r n -> r g n").bitcast(I32),
                )

        load_c_tile(0)
        nc.sync.dma_start(out=x_sc[:], in_=X_scale.rearrange("(p i) b -> p i b", i=NT))
        nc.sync.dma_start(out=x_raw[0][:], in_=x_view[:, 0, :])
        load_c_tile(1)
        nc.sync.dma_start(out=x_raw[1][:], in_=x_view[:, 1, :])
        for c in range(2, 6):
            load_c_tile(c)
        for n in range(3, 5):
            load_c_pair(n)
        load_x_quarter(1)
        load_c_pair(5)
        nc.sync.dma_start(out=amp_sb[:], in_=amp.rearrange("(g m t) -> m g t", g=NG, t=4))
        load_c_pair(6)
        load_x_quarter(2)
        load_c_pair(7)
        load_x_quarter(3)
        load_w_scales()
        for g in range(NG):
            load_w(g)
        nc.sync.dma_start(out=row_bf[:], in_=row.rearrange("(p i) -> p i", i=NT))

        x_bf, x_tr, x_grp, c_tr, c_grp = {}, {}, {}, {}, {}
        z_bank, e_tile, h_grp, y_bank = {}, {}, {}, {}

        def turn(word_sets, dummies):
            for k in range(dummies):
                bank = psum.tile([P, 512], F32, tag="bank", name="warm_bank")
                nc.tensor.matmul(bank[:], lhsT=warm[:, 0:P], rhs=warm[:], start=True, stop=True)
            tr = psum.tile([P, 2, 2, P], F32, tag="bank", name="turn_bank")
            for h in range(2):
                for u in range(2):
                    nc.tensor.transpose(tr[:, h, u, :], word_sets(h, u), ident[:])
            return tr

        def every_second_word(words):
            return lambda h, u: words[:, 256 * h + u : 256 * (h + 1) : 2]

        def copy_out(on_vector, dst, src):
            if on_vector:
                nc.vector.tensor_copy(out=dst, in_=src)
            else:
                nc.scalar.copy(out=dst, in_=src)

        def x_widen(i):
            xb = stage.tile([P, K], BF16, tag="xb", name="xb", bufs=4)
            x_bf[i] = xb
            for b in range(8):
                src = x_bytes(i)[:, P * b : P * b + P].bitcast(F8)
                if i < 2:
                    dst = xb[:, P * b : P * b + P]
                else:
                    p0 = 32 * (b % 4)
                    dst = xb[:].rearrange("p (h u m e) -> p h m u e", h=2, u=2, e=2)[:, b // 4, p0 : p0 + 32]
                    src = src.rearrange("p (m u e) -> p m u e", u=2, e=2)
                nc.vector.tensor_scalar(out=dst, in0=src, scalar1=x_sc[:, i, b : b + 1], scalar2=None, op0=MULT)

        def x_turn(i, dummies):
            words = x_bf.pop(i)[:].bitcast(F32)
            if i < 2:
                x_tr[i] = turn(every_second_word(words), dummies)
            else:
                x_tr[i] = turn(lambda h, u: words[:, 256 * h + P * u : 256 * h + P * (u + 1)], dummies)

        def x_out(i, on_vector):
            grp = stage.tile([P, 2, P, 4], BF16, tag="grp", name="x_grp_t", align_bytes=64, bufs=8)
            x_grp[i] = grp
            copy_out(on_vector, grp[:].bitcast(F32), x_tr.pop(i)[:].rearrange("p h u m -> p h m u"))

        def x_quant(i):
            grp = x_grp.pop(i)
            cols = slice(P * (i % 2), P * (i % 2) + P)
            for h in range(2):
                nc.vector.quantize_mx(
                    out=x_codes[i // 2][:, h, cols].bitcast(FP8X4),
                    scales=x_planes[i // 2][:, h, cols],
                    in_=grp[:, h, :, :].rearrange("p m j -> p (m j)"),
                )

        def c_turn(c, dummies):
            c_tr[c] = turn(every_second_word(c_rows(c).bitcast(F32)), dummies)

        def c_out(c, on_vector):
            grp = stage.tile([P, 2, P, 4], BF16, tag="grp", name="c_grp_t", align_bytes=64, bufs=8)
            c_grp[c] = grp
            copy_out(on_vector, grp[:].bitcast(F32), c_tr.pop(c)[:].rearrange("p h u m -> p h m u"))

        def c_quant(c):
            nc.vector.quantize_mx(
                out=c_codes[c][:].rearrange("p h m -> p (h m)").bitcast(FP8X4),
                scales=c_planes[c][:].rearrange("p h m -> p (h m)"),
                in_=c_grp.pop(c)[:].rearrange("p h m j -> p (h m j)"),
            )

        def first_half(q, g, a):
            z = psum.tile([P, 2, QT], F32, tag="bank", name="z_bank_t")
            z_bank[q, g, a] = z
            for b in range(2):
                c = 4 * g + 2 * a + b
                for h in range(2):
                    nc.tensor.matmul_mx(
                        out=z[:, b, :],
                        lhsT=c_codes[c][:, h, :].bitcast(FP8X4),
                        lhsT_scale=c_planes[c][:, h, :],
                        rhs=x_codes[q][:, h, :].bitcast(FP8X4),
                        rhs_scale=x_planes[q][:, h, :],
                        start=(h == 0),
                        stop=(h == 1),
                    )

        def exponential(q, g, a):
            if a == 0:
                e_tile[q, g] = stage.tile([P, 2, QT, 2], F32, tag="e", name="e_t", bufs=7)
            nc.scalar.activation(out=e_tile[q, g][:, a, :, :], in_=z_bank.pop((q, g, a))[:].rearrange("p b t -> p t b"), func=EXP)

        def times_amp(q, g, parts=1):
            hg = stage.tile([P, QT, 4], BF16, tag="h_grp", name="h_grp_t", align_bytes=64)
            h_grp[q, g] = hg
            e = e_tile.pop((q, g))
            n = QT // parts
            for t0 in range(0, QT, n):
                nc.vector.tensor_tensor(
                    out=hg[:, t0 : t0 + n, :].rearrange("p t (a b) -> p t a b", b=2),
                    in0=e[:, :, t0 : t0 + n, :].rearrange("p a t b -> p t a b"),
                    in1=amp_sb[:, g, :].rearrange("p (a b) -> p a b", b=2).unsqueeze(1).to_broadcast([P, n, 2, 2]),
                    op=MULT,
                )

        def h_quant(q, g, parts=1):
            hg = h_grp.pop((q, g))
            n = QT // parts
            for t0 in range(0, QT, n):
                nc.vector.quantize_mx(
                    out=h_codes[q][g][:, t0 : t0 + n].bitcast(FP8X4),
                    scales=h_planes[q][g][:, t0 : t0 + n],
                    in_=hg[:, t0 : t0 + n, :].rearrange("p t j -> p (t j)"),
                )

        def second_pass(bank, q, i, g, d0, width):
            nc.tensor.matmul_mx(
                out=bank,
                lhsT=h_codes[q][g][:, P * i : P * i + P].bitcast(FP8X4),
                lhsT_scale=h_planes[q][g][:, P * i : P * i + P],
                rhs=w_sb[g][:, 2 * d0 : 2 * (d0 + width)].bitcast(FP4X4),
                rhs_scale=w_sc[:, g, d0 : d0 + width],
                start=(g == 0),
                stop=(g == NG - 1),
            )

        def second_product(q, u, gs):
            if gs[0] == 0:
                y_bank[q, u] = psum.tile([P, 512], F32, tag="bank", name="y_bank_t")
            for g in gs:
                second_pass(y_bank[q, u][:], q, u // 2, g, 512 * (u % 2), 512)

        out_view = out.rearrange("(p i) d -> p i d", i=NT)

        def scale_and_store(bank, i, d0, width, engine):
            y = stage.tile([P, 512], F32, tag="y", name="y_t", bufs=8)
            if engine == "vector":
                nc.vector.tensor_scalar(out=y[:, 0:width], in0=bank, scalar1=row_sb[:, i : i + 1], scalar2=None, op0=MULT)
            else:
                nc.scalar.activation(out=y[:, 0:width], in_=bank, func=COPY, scale=row_sb[:, i : i + 1])
            nc.sync.dma_start(out=out_view[:, i, d0 : d0 + width], in_=y[:, 0:width])

        def store(q, u, engine):
            scale_and_store(y_bank.pop((q, u))[:], 2 * q + u // 2, 512 * (u % 2), 512, engine)

        def first_product(q, g):
            half_step(q, g, 0)
            half_step(q, g, 1)

        def half_step(q, g, a):
            first_half(q, g, a)
            exponential(q, g, a)

        def c_tile(c, dummies=0, on_vector=False):
            c_turn(c, dummies)
            c_out(c, on_vector)

        def x_tile(i, dummies=0, on_vector=False):
            x_turn(i, dummies)
            x_out(i, on_vector)

        def scale_and_quantise(q, g):
            times_amp(q, g)
            h_quant(q, g)

        def second_group(g):
            for u in range(4):
                second_product(0, u, [g])

        x_widen(0)
        x_widen(1)
        c_tile(0, dummies=3)
        c_tile(1, dummies=1)
        x_tile(0)
        for i in range(2):
            c_quant(i)
        x_tile(1, on_vector=True)
        for i in range(2):
            x_quant(i)
        c_tile(2, dummies=1)
        for c in range(3, 6):
            c_tile(c)
        half_step(0, 0, 0)
        for c in range(2, 6):
            c_quant(c)

        x_widen(2)
        x_widen(3)
        for c in range(6, 10):
            c_tile(c, on_vector=(c == 9))
        half_step(0, 0, 1)
        half_step(0, 1, 0)
        for c in range(6, 10):
            c_quant(c)
        scale_and_quantise(0, 0)

        c_tile(10)
        c_tile(11)
        x_tile(2)
        x_tile(3, dummies=1)
        c_tile(12)
        c_tile(13)
        x_widen(4)
        half_step(0, 1, 1)
        half_step(0, 2, 0)
        c_quant(10)
        c_quant(11)
        x_quant(2)
        x_quant(3)
        c_quant(12)
        c_quant(13)

        c_tile(14)
        c_tile(15)
        x_tile(4)
        for i in range(5, NT):
            x_widen(i)
        half_step(0, 2, 1)
        half_step(0, 3, 0)
        first_product(1, 0)
        second_group(0)
        scale_and_quantise(0, 1)
        c_quant(14)
        c_quant(15)
        x_quant(4)
        first_product(1, 1)
        half_step(0, 3, 1)
        second_group(1)
        scale_and_quantise(0, 2)

        for i in range(5, NT):
            x_tile(i)
        second_group(2)
        scale_and_quantise(0, 3)
        for i in range(5, NT):
            x_quant(i)
        nc.vector.tensor_copy(out=row_sb[:], in_=row_bf[:])

        steps = [(q, g) for q in range(1, NQ) for g in range(NG)]
        to_make, to_scale = steps[2:], steps
        units = [(q, u) for q in range(1, NQ) for u in range(4)]
        quantised, finished = 0, []
        for k, (q, g) in enumerate(to_scale):
            fresh = []
            if k < len(to_make):
                first_product(*to_make[k])
                if k == 0:
                    second_group(NG - 1)
                    fresh = [(0, u) for u in range(4)]
                elif units[0][0] <= quantised:
                    fresh = [units.pop(0)]
                    second_product(*fresh[0], range(NG))
            if g == NG - 1:
                h_quant(q, g - 1)
                times_amp(q, g, parts=2)
                h_quant(q, g, parts=2)
                quantised = q
            else:
                times_amp(q, g)
                if g > 0:
                    h_quant(q, g - 1)
            for unit in finished[:1]:
                store(*unit, "scalar")
            finished = finished[1:] + fresh

        for unit in finished:
            store(*unit, "scalar")
        while len(units) > 1:
            unit = units.pop(0)
            second_product(*unit, range(NG))
            store(*unit, "scalar")
        for d0 in (512, 768):
            bank = psum.tile([P, 256], F32, tag="bank", name="y_last")
            for g in range(NG):
                second_pass(bank[:], NQ - 1, 1, g, d0, 256)
            scale_and_store(bank[:], NT - 1, d0, 256, "scalar")
